import numpy as np
import ml_dtypes


def mxq(x, axis, fmt="e4m3"):
    dtype, down = {"e4m3": (ml_dtypes.float8_e4m3fn, 7), "e5m2": (ml_dtypes.float8_e5m2, 14)}[fmt]
    v = np.moveaxis(np.asarray(x, np.float32).astype(ml_dtypes.bfloat16).astype(np.float64), axis, -1)
    blocks = v.reshape(v.shape[:-1] + (-1, 32))
    amax = np.abs(blocks).max(-1, keepdims=True)
    byte = np.maximum(np.where(amax > 0, np.frexp(amax)[1] - 1 + 127, 0) - down, 1)
    scale = np.exp2(byte - 127.0)
    codes = (blocks / scale).astype(np.float32).astype(dtype).astype(np.float64)
    return np.moveaxis((codes * scale).reshape(v.shape), -1, axis)


WIDE = False


def mx_kscale(k):
    if not WIDE:
        return np.ones(k)
    levels = np.array([10, -10, 5, -5, 0])
    if k % 512:
        return np.exp2(np.random.permutation(np.resize(levels, k // 32))).repeat(32)
    a = np.empty((k // 512, 16))
    for p in range(k // 512):
        a[p, :8] = np.random.permutation(np.resize(levels, 8))
        for g in range(8):
            far = levels[np.abs(levels - a[p, g]) >= 10]
            a[p, g + 8] = far[np.random.randint(len(far))]
    return np.exp2(a.ravel()).repeat(32)


def f64(x):
    return np.asarray(x).astype(np.float64)


def striped(idx):
    return np.tile(np.asarray(idx).reshape(-1, 16).T, (8, 1)).astype(np.uint16)


def unstriped(offs):
    return offs[:16].T.reshape(-1).astype(np.int64)


E2M1 = np.array([0.0, 0.5, 1.0, 1.5, 2.0, 3.0, 4.0, 6.0, -0.0, -0.5, -1.0, -1.5, -2.0, -3.0, -4.0, -6.0])


def pack_weight(w, fmt):
    k, n = w.shape
    w = f64(np.asarray(w, np.float32).astype(ml_dtypes.bfloat16)).reshape(k // 32, 32, n)
    amax = np.abs(w).max(1)
    if fmt == "e4m3":
        byte = np.frexp(amax)[1] - 1 + 127 - 7
    else:
        mant, ex = np.frexp(amax / 6.0)
        byte = np.where(mant > 0.5, ex, ex - 1) + 127
    byte = np.clip(np.where(amax > 0, byte, 1), 1, 254)
    scaled = (w * np.exp2(127.0 - byte)[:, None, :]).reshape(k, n).astype(np.float32)
    by_word = np.ascontiguousarray(scaled.reshape(k // 512, 128, 4, n).transpose(0, 1, 3, 2))
    if fmt == "e4m3":
        words = by_word.astype(ml_dtypes.float8_e4m3fn).view(np.uint8)
    else:
        c = by_word.astype(ml_dtypes.float4_e2m1fn).view(np.uint8) & 0xF
        words = (c[..., 0::2] | (c[..., 1::2] << 4)).reshape(k // 512, 128, 2 * n)
    return np.ascontiguousarray(words), np.ascontiguousarray(byte.astype(np.uint8).reshape(k // 512, 16, n))


def unpack_weight(words, scales, fmt):
    g, _, n = scales.shape
    words = np.ascontiguousarray(words).reshape(g, 128, n, -1)
    if fmt == "e4m3":
        vals = words.view(ml_dtypes.float8_e4m3fn).astype(np.float64)
    else:
        nib = np.empty((g, 128, n, 4), np.uint8)
        nib[..., 0::2] = words & 0xF
        nib[..., 1::2] = words >> 4
        vals = E2M1[nib]
    vals = vals * np.repeat(np.exp2(scales.astype(np.float64) - 127.0), 8, axis=1)[..., None]
    return vals.transpose(0, 1, 3, 2).reshape(g * 512, n)


B, N, T, D, NQ = 1, 512, 2048, 1024, 256


def setup_inputs():
    n = np.random.standard_normal
    idx = np.random.permutation(T)[:B * N]
    s = mx_kscale(D)[:, None]
    kp = pack_weight(n((D, T)) / s, "e2m1")
    return {
        "qT": (n((B, D, NQ)) * s * (0.50 / np.sqrt(D))).astype(np.float32),
        "k_words": np.ascontiguousarray(kp[0].reshape(1, 2, 128, T, 2).transpose(0, 2, 3, 1, 4)).reshape(1, 128, T, 4),
        "k_scales": kp[1],
        "kb": np.tile(n(2048), (128, 1)).astype(np.float32),
        "ex": (np.random.uniform(0.5, 2.0, (B, NQ, 1))).astype(np.float32),
        "offs": striped(idx),
    }


def reference(qT, k_words, k_scales, kb, ex, offs):
    idx = unstriped(offs)
    pick = lambda x, which: x[:, which].reshape(x.shape[0], B, -1).transpose(1, 0, 2)
    k = unpack_weight(k_words.reshape(1, 128, T, 2, 2).transpose(0, 3, 1, 2, 4).reshape(2, 128, 2 * T), k_scales, "e2m1")
    kg = pick(k, idx)
    qq = mxq(f64(qT), 1, "e4m3")
    a = qq.transpose(0, 2, 1) @ kg
    y = np.exp(a + pick(f64(kb), idx)[:, :1, :]) * f64(ex)
    return y

@@ -1,0 +1,139 @@
+from contextlib import ExitStack
+
+import concourse.mybir as mybir
+from concourse.masks import make_identity
+
+T, D, NQ, N = 2048, 1024, 256, 512
+FLOPS = 2 * NQ * N * D
+BYTES = 4 * D * NQ + 4 * 128 * T + 32 * T + 4 * T + 4 * NQ + 2 * 128 * (N // 16) + 4 * NQ * N
+
+F32 = mybir.dt.float32
+BF16 = mybir.dt.bfloat16
+I32 = mybir.dt.int32
+U32 = mybir.dt.uint32
+U16 = mybir.dt.uint16
+U8 = mybir.dt.uint8
+FP8X4 = mybir.dt.float8_e4m3fn_x4
+FP4X4 = mybir.dt.float4_e2m1fn_x4
+EXP = mybir.ActivationFunctionType.Exp
+ADD = mybir.AluOpType.add
+
+P = 128
+PACK = 4
+K_PASS = P * PACK
+PASSES = D // K_PASS
+Q_BLOCKS = NQ // P
+CHUNK = 256
+KB_ROW = P - 1
+
+
+def tile_attend_rate_topk_kernel(tc, qT, k_words, k_scales, kb, ex, offs, out):
+    nc = tc.nc
+    with ExitStack() as ctx:
+        keep = ctx.enter_context(tc.tile_pool(name="keep", bufs=1))
+        psum = ctx.enter_context(tc.psum_pool(name="psum", bufs=1))
+
+        offsets = keep.tile([P, N // 16], U16, name="offsets")
+        scale_pool = keep.tile([P, PASSES, T // 4], I32, name="scale_pool", align_bytes=64)
+        kb_pool = keep.tile([P, T], F32, name="kb_pool", align_bytes=64)
+        word_pool = keep.tile([P, T], I32, name="word_pool", align_bytes=64)
+        q_raw = [keep.tile([P, PACK, NQ], F32, name=f"q_raw{o}", align_bytes=64) for o in range(PASSES)]
+        exposure = keep.tile([P, Q_BLOCKS], F32, name="exposure")
+        ident = keep.tile([P, P], F32, name="ident", align_bytes=64)
+        warm_in = keep.tile([P, 1], F32, name="warm_in")
+        warm_out = keep.tile([P, 1], F32, name="warm_out")
+
+        nc.vector.memset(scale_pool[:], 0)
+        nc.vector.memset(kb_pool[0:KB_ROW, :], 0.0)
+        nc.gpsimd.memset(warm_in[:], 0.0)
+        nc.scalar.activation(out=warm_out[:], in_=warm_in[:], func=EXP)
+        make_identity(nc, ident[:])
+
+        def load_queries(o):
+            rows = qT[0, o * K_PASS : (o + 1) * K_PASS, :]
+            nc.sync.dma_start(out=q_raw[o][:], in_=rows.rearrange("(p j) q -> p j q", j=PACK))
+
+        nc.sync.dma_start(offsets[:], offs)
+        nc.sync.dma_start(out=kb_pool[KB_ROW:P, :], in_=kb[0:1, :])
+        load_queries(0)
+        scale_rows = k_scales.bitcast(I32)
+        for r in range(4):
+            nc.sync.dma_start(
+                out=scale_pool[r:P:32, :, :],
+                in_=scale_rows[:, r:16:4, :].rearrange("o g t -> g o t"),
+            )
+        nc.sync.dma_start(out=word_pool[:], in_=k_words[0].rearrange("p t b -> p (t b)").bitcast(I32))
+        load_queries(1)
+        with nc.allow_non_contiguous_dma(reason="one exposure a query row"):
+            nc.sync.dma_start(out=exposure[:], in_=ex[0].rearrange("(c p) one -> p (c one)", p=P))
+
+        kb_row = keep.tile([P, N], F32, name="kb_row", align_bytes=64)
+        nc.vector.tensor_copy(out=kb_row[:], in_=kb_pool[:].indirect(offsets[:]))
+        turned = psum.tile([P, N // P, P], F32, name="turned")
+        for j in range(N // P):
+            nc.tensor.transpose(turned[:, j, :], kb_row[:, j * P : (j + 1) * P], ident[:])
+        kb_cols = keep.tile([P, N // P], F32, name="kb_cols", align_bytes=64)
+        nc.scalar.copy(out=kb_cols[:], in_=turned[:, :, KB_ROW])
+        spread = psum.tile([P, N], F32, name="spread")
+        for j in range(N // P):
+            nc.tensor.transpose(spread[:, j * P : (j + 1) * P], kb_cols[:, j : j + 1].to_broadcast([P, P]), ident[:])
+        bias = keep.tile([P, N], F32, name="bias", align_bytes=64)
+        nc.scalar.copy(out=bias[:], in_=spread[:])
+
+        q_bf = keep.tile([P, PASSES, NQ, PACK], BF16, name="q_bf", align_bytes=64)
+        q_codes = keep.tile([P, PASSES, NQ], U32, name="q_codes", align_bytes=64)
+        q_scales = keep.tile([P, PASSES, NQ], U8, name="q_scales", align_bytes=64)
+
+        def interleave(engine_copy, o, cols):
+            engine_copy(out=q_bf[:, o, cols, :], in_=q_raw[o][:, :, cols].rearrange("p j q -> p q j"))
+
+        def quantize(o, cols):
+            nc.vector.quantize_mx(
+                out=q_codes[:, o, cols].bitcast(FP8X4),
+                scales=q_scales[:, o, cols],
+                in_=q_bf[:, o, cols, :].rearrange("p q j -> p (q j)"),
+            )
+
+        blocks = [slice(c * P, (c + 1) * P) for c in range(Q_BLOCKS)]
+        interleave(nc.scalar.copy, 0, slice(0, NQ))
+
+        key_scales = keep.tile([P, PASSES, N], U8, name="key_scales", align_bytes=64)
+        for o in range(PASSES):
+            nc.vector.tensor_copy(out=key_scales[:, o, :], in_=scale_pool[:, o, :].bitcast(U8).indirect(offsets[:]))
+        quantize(0, slice(0, NQ))
+
+        word_pairs = keep.tile([P, N], U32, name="word_pairs", align_bytes=64)
+        nc.vector.tensor_copy(out=word_pairs[:], in_=word_pool[:].bitcast(U32).indirect(offsets[:]))
+        key_words = keep.tile([P, PASSES, 2 * N], U8, name="key_words", align_bytes=64)
+        halves = word_pairs[:].bitcast(U16).rearrange("p (i o) -> p o i", o=PASSES)
+        for o in range(PASSES):
+            nc.vector.tensor_copy(out=key_words[:, o, :].bitcast(U16), in_=halves[:, o, :])
+
+        interleave(nc.scalar.copy, 1, blocks[1])
+        interleave(nc.vector.tensor_copy, 1, blocks[0])
+        quantize(1, blocks[0])
+        quantize(1, blocks[1])
+
+        scores = [psum.tile([P, N], F32, name=f"scores{c}") for c in range(Q_BLOCKS)]
+        for o in range(PASSES):
+            for c in range(Q_BLOCKS):
+                nc.tensor.matmul_mx(
+                    out=scores[c][:],
+                    lhsT=q_codes[:, o, blocks[c]].bitcast(FP8X4),
+                    lhsT_scale=q_scales[:, o, blocks[c]],
+                    rhs=key_words[:, o, :].bitcast(FP4X4),
+                    rhs_scale=key_scales[:, o, :],
+                    start=(o == 0),
+                    stop=(o == PASSES - 1),
+                )
+
+        for c in range(Q_BLOCKS):
+            for h in range(N // CHUNK):
+                cols = slice(h * CHUNK, (h + 1) * CHUNK)
+                logit = keep.tile([P, CHUNK], F32, name=f"logit{c}{h}", align_bytes=64)
+                rate = keep.tile([P, CHUNK], F32, name=f"rate{c}{h}", align_bytes=64)
+                result = keep.tile([P, CHUNK], F32, name=f"result{c}{h}", align_bytes=64)
+                nc.vector.tensor_tensor(out=logit[:], in0=scores[c][:, cols], in1=bias[:, cols], op=ADD)
+                nc.scalar.activation(out=rate[:], in_=logit[:], func=EXP)
+                nc.vector.tensor_scalar_mul(out=result[:], in0=rate[:], scalar1=exposure[:, c : c + 1])
+                nc.sync.dma_start(out=out[0, blocks[c], cols], in_=result[:])

@@ -23,7 +23,6 @@ PACK = 4
 K_PASS = P * PACK
 PASSES = D // K_PASS
 Q_BLOCKS = NQ // P
-CHUNK = 256
 KB_ROW = P - 1
 
 
@@ -34,7 +33,7 @@ def tile_attend_rate_topk_kernel(tc, qT, k_words, k_scales, kb, ex, offs, out):
         psum = ctx.enter_context(tc.psum_pool(name="psum", bufs=1))
 
         offsets = keep.tile([P, N // 16], U16, name="offsets")
-        scale_pool = keep.tile([P, PASSES, T // 4], I32, name="scale_pool", align_bytes=64)
+        scale_pool = keep.tile([P, T // 4], I32, name="scale_pool", align_bytes=64)
         kb_pool = keep.tile([P, T], F32, name="kb_pool", align_bytes=64)
         word_pool = keep.tile([P, T], I32, name="word_pool", align_bytes=64)
         q_raw = [keep.tile([P, PACK, NQ], F32, name=f"q_raw{o}", align_bytes=64) for o in range(PASSES)]
@@ -42,30 +41,36 @@ def tile_attend_rate_topk_kernel(tc, qT, k_words, k_scales, kb, ex, offs, out):
         ident = keep.tile([P, P], F32, name="ident", align_bytes=64)
         warm_in = keep.tile([P, 1], F32, name="warm_in")
         warm_out = keep.tile([P, 1], F32, name="warm_out")
+        moved_scales = keep.tile([P, N // 4], I32, name="moved_scales", align_bytes=64)
 
-        nc.vector.memset(scale_pool[:], 0)
-        nc.vector.memset(kb_pool[0:KB_ROW, :], 0.0)
+        nc.gpsimd.memset(scale_pool[:], 0)
         nc.gpsimd.memset(warm_in[:], 0.0)
-        nc.scalar.activation(out=warm_out[:], in_=warm_in[:], func=EXP)
+        nc.vector.memset(kb_pool[0:KB_ROW, :], 0.0)
+        nc.vector.memset(moved_scales[:], 0)
         make_identity(nc, ident[:])
-
-        def load_queries(o):
-            rows = qT[0, o * K_PASS : (o + 1) * K_PASS, :]
-            nc.sync.dma_start(out=q_raw[o][:], in_=rows.rearrange("(p j) q -> p j q", j=PACK))
 
         nc.sync.dma_start(offsets[:], offs)
         nc.sync.dma_start(out=kb_pool[KB_ROW:P, :], in_=kb[0:1, :])
-        load_queries(0)
         scale_rows = k_scales.bitcast(I32)
+        nc.sync.dma_start(out=scale_pool[4:20, :], in_=scale_rows[1])
         for r in range(4):
-            nc.sync.dma_start(
-                out=scale_pool[r:P:32, :, :],
-                in_=scale_rows[:, r:16:4, :].rearrange("o g t -> g o t"),
-            )
+            nc.sync.dma_start(out=scale_pool[r:P:32, :], in_=scale_rows[0, r:16:4, :])
+        nc.scalar.activation(out=warm_out[:], in_=warm_in[:], func=EXP)
         nc.sync.dma_start(out=word_pool[:], in_=k_words[0].rearrange("p t b -> p (t b)").bitcast(I32))
-        load_queries(1)
+        for o in range(PASSES):
+            rows = qT[0, o * K_PASS : (o + 1) * K_PASS, :]
+            nc.sync.dma_start(out=q_raw[o][:], in_=rows.rearrange("(p j) q -> p j q", j=PACK))
         with nc.allow_non_contiguous_dma(reason="one exposure a query row"):
             nc.sync.dma_start(out=exposure[:], in_=ex[0].rearrange("(c p) one -> p (c one)", p=P))
+
+        listed_scales = keep.tile([P, N], U8, name="listed_scales", align_bytes=64)
+        nc.vector.tensor_copy(out=listed_scales[:], in_=scale_pool[:].bitcast(U8).indirect(offsets[:]))
+        for g in range(4):
+            nc.scalar.dma_start(
+                out=moved_scales[32 * g : 32 * g + 4, :],
+                in_=listed_scales[4 + 4 * g : 8 + 4 * g, :].bitcast(I32),
+            )
+        key_scales = [listed_scales[:], moved_scales[:].bitcast(U8)]
 
         kb_row = keep.tile([P, N], F32, name="kb_row", align_bytes=64)
         nc.vector.tensor_copy(out=kb_row[:], in_=kb_pool[:].indirect(offsets[:]))
@@ -80,60 +85,49 @@ def tile_attend_rate_topk_kernel(tc, qT, k_words, k_scales, kb, ex, offs, out):
         bias = keep.tile([P, N], F32, name="bias", align_bytes=64)
         nc.scalar.copy(out=bias[:], in_=spread[:])
 
-        q_bf = keep.tile([P, PASSES, NQ, PACK], BF16, name="q_bf", align_bytes=64)
-        q_codes = keep.tile([P, PASSES, NQ], U32, name="q_codes", align_bytes=64)
-        q_scales = keep.tile([P, PASSES, NQ], U8, name="q_scales", align_bytes=64)
-
-        def interleave(engine_copy, o, cols):
-            engine_copy(out=q_bf[:, o, cols, :], in_=q_raw[o][:, :, cols].rearrange("p j q -> p q j"))
-
-        def quantize(o, cols):
-            nc.vector.quantize_mx(
-                out=q_codes[:, o, cols].bitcast(FP8X4),
-                scales=q_scales[:, o, cols],
-                in_=q_bf[:, o, cols, :].rearrange("p q j -> p (q j)"),
-            )
-
-        blocks = [slice(c * P, (c + 1) * P) for c in range(Q_BLOCKS)]
-        interleave(nc.scalar.copy, 0, slice(0, NQ))
-
-        key_scales = keep.tile([P, PASSES, N], U8, name="key_scales", align_bytes=64)
-        for o in range(PASSES):
-            nc.vector.tensor_copy(out=key_scales[:, o, :], in_=scale_pool[:, o, :].bitcast(U8).indirect(offsets[:]))
-        quantize(0, slice(0, NQ))
-
         word_pairs = keep.tile([P, N], U32, name="word_pairs", align_bytes=64)
         nc.vector.tensor_copy(out=word_pairs[:], in_=word_pool[:].bitcast(U32).indirect(offsets[:]))
-        key_words = keep.tile([P, PASSES, 2 * N], U8, name="key_words", align_bytes=64)
         halves = word_pairs[:].bitcast(U16).rearrange("p (i o) -> p o i", o=PASSES)
-        for o in range(PASSES):
-            nc.vector.tensor_copy(out=key_words[:, o, :].bitcast(U16), in_=halves[:, o, :])
-
-        interleave(nc.scalar.copy, 1, blocks[1])
-        interleave(nc.vector.tensor_copy, 1, blocks[0])
-        quantize(1, blocks[0])
-        quantize(1, blocks[1])
-
+        blocks = [slice(c * P, (c + 1) * P) for c in range(Q_BLOCKS)]
         scores = [psum.tile([P, N], F32, name=f"scores{c}") for c in range(Q_BLOCKS)]
-        for o in range(PASSES):
-            for c in range(Q_BLOCKS):
-                nc.tensor.matmul_mx(
-                    out=scores[c][:],
-                    lhsT=q_codes[:, o, blocks[c]].bitcast(FP8X4),
-                    lhsT_scale=q_scales[:, o, blocks[c]],
-                    rhs=key_words[:, o, :].bitcast(FP4X4),
-                    rhs_scale=key_scales[:, o, :],
-                    start=(o == 0),
-                    stop=(o == PASSES - 1),
-                )
+        key_words = [keep.tile([P, 2 * N], U8, name=f"key_words{o}", align_bytes=64) for o in range(PASSES)]
 
-        for c in range(Q_BLOCKS):
-            for h in range(N // CHUNK):
-                cols = slice(h * CHUNK, (h + 1) * CHUNK)
-                logit = keep.tile([P, CHUNK], F32, name=f"logit{c}{h}", align_bytes=64)
-                rate = keep.tile([P, CHUNK], F32, name=f"rate{c}{h}", align_bytes=64)
-                result = keep.tile([P, CHUNK], F32, name=f"result{c}{h}", align_bytes=64)
-                nc.vector.tensor_tensor(out=logit[:], in0=scores[c][:, cols], in1=bias[:, cols], op=ADD)
-                nc.scalar.activation(out=rate[:], in_=logit[:], func=EXP)
-                nc.vector.tensor_scalar_mul(out=result[:], in0=rate[:], scalar1=exposure[:, c : c + 1])
-                nc.sync.dma_start(out=out[0, blocks[c], cols], in_=result[:])
+        def part_words(o):
+            nc.vector.tensor_copy(out=key_words[o][:].bitcast(U16), in_=halves[:, o, :])
+
+        def score(o, c, copy):
+            q_bf = keep.tile([P, P, PACK], BF16, name=f"q_bf{o}{c}", align_bytes=64)
+            q_codes = keep.tile([P, P], U32, name=f"q_codes{o}{c}", align_bytes=64)
+            q_scales = keep.tile([P, P], U8, name=f"q_scales{o}{c}", align_bytes=64)
+            copy(out=q_bf[:], in_=q_raw[o][:, :, blocks[c]].rearrange("p j q -> p q j"))
+            nc.vector.quantize_mx(
+                out=q_codes[:].bitcast(FP8X4),
+                scales=q_scales[:],
+                in_=q_bf[:].rearrange("p q j -> p (q j)"),
+            )
+            nc.tensor.matmul_mx(
+                out=scores[c][:],
+                lhsT=q_codes[:].bitcast(FP8X4),
+                lhsT_scale=q_scales[:],
+                rhs=key_words[o][:].bitcast(FP4X4),
+                rhs_scale=key_scales[o],
+                start=(o == 0),
+                stop=(o == PASSES - 1),
+            )
+
+        part_words(0)
+        score(0, 0, nc.scalar.copy)
+        score(0, 1, nc.scalar.copy)
+        part_words(1)
+        score(1, 0, nc.vector.tensor_copy)
+        score(1, 1, nc.scalar.copy)
+
+        for c, lo, hi in ((0, 0, 256), (0, 256, 512), (1, 0, 256), (1, 256, 384), (1, 384, 512)):
+            cols = slice(lo, hi)
+            logit = keep.tile([P, hi - lo], F32, name=f"logit{c}{lo}", align_bytes=64)
+            rate = keep.tile([P, hi - lo], F32, name=f"rate{c}{lo}", align_bytes=64)
+            result = keep.tile([P, hi - lo], F32, name=f"result{c}{lo}", align_bytes=64)
+            nc.vector.tensor_tensor(out=logit[:], in0=scores[c][:, cols], in1=bias[:, cols], op=ADD)
+            nc.scalar.activation(out=rate[:], in_=logit[:], func=EXP)
+            nc.vector.tensor_scalar_mul(out=result[:], in0=rate[:], scalar1=exposure[:, c : c + 1])
+            nc.sync.dma_start(out=out[0, blocks[c], cols], in_=result[:])

@@ -23,7 +23,11 @@ PACK = 4
 K_PASS = P * PACK
 PASSES = D // K_PASS
 Q_BLOCKS = NQ // P
+QUADRANT = 32
+GROUP = 4
+SPARE_ROW = GROUP
 KB_ROW = P - 1
+PIECES = ((0, 0, 256), (0, 256, 512), (1, 0, 256), (1, 256, 384), (1, 384, 512))
 
 
 def tile_attend_rate_topk_kernel(tc, qT, k_words, k_scales, kb, ex, offs, out):
@@ -36,25 +40,25 @@ def tile_attend_rate_topk_kernel(tc, qT, k_words, k_scales, kb, ex, offs, out):
         scale_pool = keep.tile([P, T // 4], I32, name="scale_pool", align_bytes=64)
         kb_pool = keep.tile([P, T], F32, name="kb_pool", align_bytes=64)
         word_pool = keep.tile([P, T], I32, name="word_pool", align_bytes=64)
-        q_raw = [keep.tile([P, PACK, NQ], F32, name=f"q_raw{o}", align_bytes=64) for o in range(PASSES)]
+        q_raw = [keep.tile([P, PACK, NQ], F32, name=f"q_raw{o}", tag=f"stage{o}", align_bytes=64) for o in range(PASSES)]
         exposure = keep.tile([P, Q_BLOCKS], F32, name="exposure")
         ident = keep.tile([P, P], F32, name="ident", align_bytes=64)
         warm_in = keep.tile([P, 1], F32, name="warm_in")
         warm_out = keep.tile([P, 1], F32, name="warm_out")
-        moved_scales = keep.tile([P, N // 4], I32, name="moved_scales", align_bytes=64)
+        pass1_plane = keep.tile([P, N // 4], I32, name="pass1_plane", align_bytes=64)
 
         nc.gpsimd.memset(scale_pool[:], 0)
         nc.gpsimd.memset(warm_in[:], 0.0)
         nc.vector.memset(kb_pool[0:KB_ROW, :], 0.0)
-        nc.vector.memset(moved_scales[:], 0)
+        nc.vector.memset(pass1_plane[:], 0)
         make_identity(nc, ident[:])
 
         nc.sync.dma_start(offsets[:], offs)
         nc.sync.dma_start(out=kb_pool[KB_ROW:P, :], in_=kb[0:1, :])
         scale_rows = k_scales.bitcast(I32)
-        nc.sync.dma_start(out=scale_pool[4:20, :], in_=scale_rows[1])
-        for r in range(4):
-            nc.sync.dma_start(out=scale_pool[r:P:32, :], in_=scale_rows[0, r:16:4, :])
+        nc.scalar.dma_start(out=scale_pool[SPARE_ROW : SPARE_ROW + GROUP * GROUP, :], in_=scale_rows[1])
+        for r in range(GROUP):
+            nc.sync.dma_start(out=scale_pool[r:P:QUADRANT, :], in_=scale_rows[0, r : GROUP * GROUP : GROUP, :])
         nc.scalar.activation(out=warm_out[:], in_=warm_in[:], func=EXP)
         nc.sync.dma_start(out=word_pool[:], in_=k_words[0].rearrange("p t b -> p (t b)").bitcast(I32))
         for o in range(PASSES):
@@ -65,12 +69,13 @@ def tile_attend_rate_topk_kernel(tc, qT, k_words, k_scales, kb, ex, offs, out):
 
         listed_scales = keep.tile([P, N], U8, name="listed_scales", align_bytes=64)
         nc.vector.tensor_copy(out=listed_scales[:], in_=scale_pool[:].bitcast(U8).indirect(offsets[:]))
-        for g in range(4):
+        for g in range(GROUP):
+            first = SPARE_ROW + GROUP * g
             nc.scalar.dma_start(
-                out=moved_scales[32 * g : 32 * g + 4, :],
-                in_=listed_scales[4 + 4 * g : 8 + 4 * g, :].bitcast(I32),
+                out=pass1_plane[QUADRANT * g : QUADRANT * g + GROUP, :],
+                in_=listed_scales[first : first + GROUP, :].bitcast(I32),
             )
-        key_scales = [listed_scales[:], moved_scales[:].bitcast(U8)]
+        key_scales = [listed_scales[:], pass1_plane[:].bitcast(U8)]
 
         kb_row = keep.tile([P, N], F32, name="kb_row", align_bytes=64)
         nc.vector.tensor_copy(out=kb_row[:], in_=kb_pool[:].indirect(offsets[:]))
@@ -82,8 +87,6 @@ def tile_attend_rate_topk_kernel(tc, qT, k_words, k_scales, kb, ex, offs, out):
         spread = psum.tile([P, N], F32, name="spread")
         for j in range(N // P):
             nc.tensor.transpose(spread[:, j * P : (j + 1) * P], kb_cols[:, j : j + 1].to_broadcast([P, P]), ident[:])
-        bias = keep.tile([P, N], F32, name="bias", align_bytes=64)
-        nc.scalar.copy(out=bias[:], in_=spread[:])
 
         word_pairs = keep.tile([P, N], U32, name="word_pairs", align_bytes=64)
         nc.vector.tensor_copy(out=word_pairs[:], in_=word_pool[:].bitcast(U32).indirect(offsets[:]))
@@ -122,7 +125,10 @@ def tile_attend_rate_topk_kernel(tc, qT, k_words, k_scales, kb, ex, offs, out):
         score(1, 0, nc.vector.tensor_copy)
         score(1, 1, nc.scalar.copy)
 
-        for c, lo, hi in ((0, 0, 256), (0, 256, 512), (1, 0, 256), (1, 256, 384), (1, 384, 512)):
+        bias = keep.tile([P, N], F32, name="bias", tag="stage1", align_bytes=64)
+        nc.scalar.copy(out=bias[:], in_=spread[:])
+
+        for c, lo, hi in PIECES:
             cols = slice(lo, hi)
             logit = keep.tile([P, hi - lo], F32, name=f"logit{c}{lo}", align_bytes=64)
             rate = keep.tile([P, hi - lo], F32, name=f"rate{c}{lo}", align_bytes=64)

@@ -25,8 +25,9 @@ PASSES = D // K_PASS
 Q_BLOCKS = NQ // P
 QUADRANT = 32
 GROUP = 4
-SPARE_ROW = GROUP
+SHIFT = QUADRANT // 2
 KB_ROW = P - 1
+VECTOR_SHARE = 64
 PIECES = ((0, 0, 256), (0, 256, 512), (1, 0, 256), (1, 256, 384), (1, 384, 512))
 
 
@@ -50,15 +51,15 @@ def tile_attend_rate_topk_kernel(tc, qT, k_words, k_scales, kb, ex, offs, out):
         nc.gpsimd.memset(scale_pool[:], 0)
         nc.gpsimd.memset(warm_in[:], 0.0)
         nc.vector.memset(kb_pool[0:KB_ROW, :], 0.0)
-        nc.vector.memset(pass1_plane[:], 0)
+        nc.gpsimd.memset(pass1_plane[:], 0)
         make_identity(nc, ident[:])
 
-        nc.sync.dma_start(offsets[:], offs)
         nc.sync.dma_start(out=kb_pool[KB_ROW:P, :], in_=kb[0:1, :])
-        scale_rows = k_scales.bitcast(I32)
-        nc.scalar.dma_start(out=scale_pool[SPARE_ROW : SPARE_ROW + GROUP * GROUP, :], in_=scale_rows[1])
+        nc.sync.dma_start(offsets[:], offs)
+        scale_rows = k_scales.bitcast(I32).rearrange("o (g r) t -> r g o t", r=GROUP)
         for r in range(GROUP):
-            nc.sync.dma_start(out=scale_pool[r:P:QUADRANT, :], in_=scale_rows[0, r : GROUP * GROUP : GROUP, :])
+            queue = nc.sync if r % 2 == 0 else nc.scalar
+            queue.dma_start(out=scale_pool[r:P:SHIFT, :], in_=scale_rows[r])
         nc.scalar.activation(out=warm_out[:], in_=warm_in[:], func=EXP)
         nc.sync.dma_start(out=word_pool[:], in_=k_words[0].rearrange("p t b -> p (t b)").bitcast(I32))
         for o in range(PASSES):
@@ -70,36 +71,41 @@ def tile_attend_rate_topk_kernel(tc, qT, k_words, k_scales, kb, ex, offs, out):
         listed_scales = keep.tile([P, N], U8, name="listed_scales", align_bytes=64)
         nc.vector.tensor_copy(out=listed_scales[:], in_=scale_pool[:].bitcast(U8).indirect(offsets[:]))
         for g in range(GROUP):
-            first = SPARE_ROW + GROUP * g
+            first = QUADRANT * g
             nc.scalar.dma_start(
-                out=pass1_plane[QUADRANT * g : QUADRANT * g + GROUP, :],
-                in_=listed_scales[first : first + GROUP, :].bitcast(I32),
+                out=pass1_plane[first : first + GROUP, :],
+                in_=listed_scales[first + SHIFT : first + SHIFT + GROUP, :].bitcast(I32),
             )
         key_scales = [listed_scales[:], pass1_plane[:].bitcast(U8)]
 
-        kb_row = keep.tile([P, N], F32, name="kb_row", align_bytes=64)
+        kb_row = keep.tile([P, N], F32, name="kb_row", tag="gathered", align_bytes=64)
         nc.vector.tensor_copy(out=kb_row[:], in_=kb_pool[:].indirect(offsets[:]))
         turned = psum.tile([P, N // P, P], F32, name="turned")
         for j in range(N // P):
             nc.tensor.transpose(turned[:, j, :], kb_row[:, j * P : (j + 1) * P], ident[:])
         kb_cols = keep.tile([P, N // P], F32, name="kb_cols", align_bytes=64)
-        nc.scalar.copy(out=kb_cols[:], in_=turned[:, :, KB_ROW])
+        nc.vector.tensor_copy(out=kb_cols[:], in_=turned[:, :, KB_ROW])
         spread = psum.tile([P, N], F32, name="spread")
         for j in range(N // P):
             nc.tensor.transpose(spread[:, j * P : (j + 1) * P], kb_cols[:, j : j + 1].to_broadcast([P, P]), ident[:])
 
-        word_pairs = keep.tile([P, N], U32, name="word_pairs", align_bytes=64)
+        word_pairs = keep.tile([P, N], U32, name="word_pairs", tag="gathered", align_bytes=64)
         nc.vector.tensor_copy(out=word_pairs[:], in_=word_pool[:].bitcast(U32).indirect(offsets[:]))
         halves = word_pairs[:].bitcast(U16).rearrange("p (i o) -> p o i", o=PASSES)
         blocks = [slice(c * P, (c + 1) * P) for c in range(Q_BLOCKS)]
         scores = [psum.tile([P, N], F32, name=f"scores{c}") for c in range(Q_BLOCKS)]
-        key_words = [keep.tile([P, 2 * N], U8, name=f"key_words{o}", align_bytes=64) for o in range(PASSES)]
+        key_words = {}
 
-        def part_words(o):
+        def part_words(o, tag):
+            key_words[o] = keep.tile([P, 2 * N], U8, name=f"key_words{o}", tag=tag, align_bytes=64)
             nc.vector.tensor_copy(out=key_words[o][:].bitcast(U16), in_=halves[:, o, :])
 
+        def shared_copy(out, in_):
+            nc.vector.tensor_copy(out=out[:, 0:VECTOR_SHARE, :], in_=in_[:, 0:VECTOR_SHARE, :])
+            nc.scalar.copy(out=out[:, VECTOR_SHARE:P, :], in_=in_[:, VECTOR_SHARE:P, :])
+
         def score(o, c, copy):
-            q_bf = keep.tile([P, P, PACK], BF16, name=f"q_bf{o}{c}", align_bytes=64)
+            q_bf = keep.tile([P, P, PACK], BF16, name=f"q_bf{o}{c}", tag=f"rounded{o}{c}", align_bytes=64)
             q_codes = keep.tile([P, P], U32, name=f"q_codes{o}{c}", align_bytes=64)
             q_scales = keep.tile([P, P], U8, name=f"q_scales{o}{c}", align_bytes=64)
             copy(out=q_bf[:], in_=q_raw[o][:, :, blocks[c]].rearrange("p j q -> p q j"))
@@ -118,12 +124,12 @@ def tile_attend_rate_topk_kernel(tc, qT, k_words, k_scales, kb, ex, offs, out):
                 stop=(o == PASSES - 1),
             )
 
-        part_words(0)
+        part_words(0, "words0")
         score(0, 0, nc.scalar.copy)
         score(0, 1, nc.scalar.copy)
-        part_words(1)
-        score(1, 0, nc.vector.tensor_copy)
-        score(1, 1, nc.scalar.copy)
+        part_words(1, "words1")
+        score(1, 0, shared_copy)
+        score(1, 1, shared_copy)
 
         bias = keep.tile([P, N], F32, name="bias", tag="stage1", align_bytes=64)
         nc.scalar.copy(out=bias[:], in_=spread[:])

@@ -25,10 +25,11 @@ PASSES = D // K_PASS
 Q_BLOCKS = NQ // P
 QUADRANT = 32
 GROUP = 4
-SHIFT = QUADRANT // 2
+SPARE_ROW = GROUP
 KB_ROW = P - 1
 VECTOR_SHARE = 64
-PIECES = ((0, 0, 256), (0, 256, 512), (1, 0, 256), (1, 256, 384), (1, 384, 512))
+LINE = 4
+PIECES = ((0, 0, 128), (0, 128, 256), (0, 256, 512), (1, 0, 256), (1, 256, 384), (1, 384, 512))
 
 
 def tile_attend_rate_topk_kernel(tc, qT, k_words, k_scales, kb, ex, offs, out):
@@ -50,16 +51,16 @@ def tile_attend_rate_topk_kernel(tc, qT, k_words, k_scales, kb, ex, offs, out):
 
         nc.gpsimd.memset(scale_pool[:], 0)
         nc.gpsimd.memset(warm_in[:], 0.0)
-        nc.vector.memset(kb_pool[0:KB_ROW, :], 0.0)
-        nc.gpsimd.memset(pass1_plane[:], 0)
         make_identity(nc, ident[:])
+        nc.vector.memset(kb_pool[0:KB_ROW, :], 0.0)
+        nc.vector.memset(pass1_plane[:], 0)
 
         nc.sync.dma_start(out=kb_pool[KB_ROW:P, :], in_=kb[0:1, :])
         nc.sync.dma_start(offsets[:], offs)
-        scale_rows = k_scales.bitcast(I32).rearrange("o (g r) t -> r g o t", r=GROUP)
+        scale_rows = k_scales.bitcast(I32)
+        nc.scalar.dma_start(out=scale_pool[SPARE_ROW : SPARE_ROW + GROUP * GROUP, :], in_=scale_rows[1])
         for r in range(GROUP):
-            queue = nc.sync if r % 2 == 0 else nc.scalar
-            queue.dma_start(out=scale_pool[r:P:SHIFT, :], in_=scale_rows[r])
+            nc.sync.dma_start(out=scale_pool[r:P:QUADRANT, :], in_=scale_rows[0, r : GROUP * GROUP : GROUP, :])
         nc.scalar.activation(out=warm_out[:], in_=warm_in[:], func=EXP)
         nc.sync.dma_start(out=word_pool[:], in_=k_words[0].rearrange("p t b -> p (t b)").bitcast(I32))
         for o in range(PASSES):
@@ -68,32 +69,36 @@ def tile_attend_rate_topk_kernel(tc, qT, k_words, k_scales, kb, ex, offs, out):
         with nc.allow_non_contiguous_dma(reason="one exposure a query row"):
             nc.sync.dma_start(out=exposure[:], in_=ex[0].rearrange("(c p) one -> p (c one)", p=P))
 
+        kb_row = keep.tile([P, N], F32, name="kb_row", align_bytes=64)
+        nc.vector.tensor_copy(out=kb_row[:], in_=kb_pool[:].indirect(offsets[:]))
+
         listed_scales = keep.tile([P, N], U8, name="listed_scales", align_bytes=64)
         nc.vector.tensor_copy(out=listed_scales[:], in_=scale_pool[:].bitcast(U8).indirect(offsets[:]))
         for g in range(GROUP):
-            first = QUADRANT * g
+            first = SPARE_ROW + GROUP * g
             nc.scalar.dma_start(
-                out=pass1_plane[first : first + GROUP, :],
-                in_=listed_scales[first + SHIFT : first + SHIFT + GROUP, :].bitcast(I32),
+                out=pass1_plane[QUADRANT * g : QUADRANT * g + GROUP, :],
+                in_=listed_scales[first : first + GROUP, :].bitcast(I32),
             )
         key_scales = [listed_scales[:], pass1_plane[:].bitcast(U8)]
 
-        kb_row = keep.tile([P, N], F32, name="kb_row", tag="gathered", align_bytes=64)
-        nc.vector.tensor_copy(out=kb_row[:], in_=kb_pool[:].indirect(offsets[:]))
         turned = psum.tile([P, N // P, P], F32, name="turned")
         for j in range(N // P):
             nc.tensor.transpose(turned[:, j, :], kb_row[:, j * P : (j + 1) * P], ident[:])
         kb_cols = keep.tile([P, N // P], F32, name="kb_cols", align_bytes=64)
-        nc.vector.tensor_copy(out=kb_cols[:], in_=turned[:, :, KB_ROW])
+        nc.scalar.copy(out=kb_cols[:], in_=turned[:, :, KB_ROW])
         spread = psum.tile([P, N], F32, name="spread")
         for j in range(N // P):
             nc.tensor.transpose(spread[:, j * P : (j + 1) * P], kb_cols[:, j : j + 1].to_broadcast([P, P]), ident[:])
 
-        word_pairs = keep.tile([P, N], U32, name="word_pairs", tag="gathered", align_bytes=64)
+        word_pairs = keep.tile([P, N], U32, name="word_pairs", align_bytes=64)
         nc.vector.tensor_copy(out=word_pairs[:], in_=word_pool[:].bitcast(U32).indirect(offsets[:]))
         halves = word_pairs[:].bitcast(U16).rearrange("p (i o) -> p o i", o=PASSES)
         blocks = [slice(c * P, (c + 1) * P) for c in range(Q_BLOCKS)]
-        scores = [psum.tile([P, N], F32, name=f"scores{c}") for c in range(Q_BLOCKS)]
+        widths = (P, N)
+        scores = [
+            [psum.tile([P, widths[c]], F32, name=f"scores{c}{j}") for j in range(N // widths[c])] for c in range(Q_BLOCKS)
+        ]
         key_words = {}
 
         def part_words(o, tag):
@@ -101,28 +106,34 @@ def tile_attend_rate_topk_kernel(tc, qT, k_words, k_scales, kb, ex, offs, out):
             nc.vector.tensor_copy(out=key_words[o][:].bitcast(U16), in_=halves[:, o, :])
 
         def shared_copy(out, in_):
-            nc.vector.tensor_copy(out=out[:, 0:VECTOR_SHARE, :], in_=in_[:, 0:VECTOR_SHARE, :])
-            nc.scalar.copy(out=out[:, VECTOR_SHARE:P, :], in_=in_[:, VECTOR_SHARE:P, :])
+            runs = VECTOR_SHARE // LINE
+            nc.vector.tensor_copy(out=out[:, 0:runs], in_=in_[:, 0:runs])
+            nc.scalar.copy(out=out[:, runs : P // LINE], in_=in_[:, runs : P // LINE])
 
         def score(o, c, copy):
             q_bf = keep.tile([P, P, PACK], BF16, name=f"q_bf{o}{c}", tag=f"rounded{o}{c}", align_bytes=64)
             q_codes = keep.tile([P, P], U32, name=f"q_codes{o}{c}", align_bytes=64)
             q_scales = keep.tile([P, P], U8, name=f"q_scales{o}{c}", align_bytes=64)
-            copy(out=q_bf[:], in_=q_raw[o][:, :, blocks[c]].rearrange("p j q -> p q j"))
+            copy(
+                out=q_bf[:].rearrange("p (a i) j -> p a j i", i=LINE),
+                in_=q_raw[o][:, :, blocks[c]].rearrange("p j (a i) -> p a j i", i=LINE),
+            )
             nc.vector.quantize_mx(
                 out=q_codes[:].bitcast(FP8X4),
                 scales=q_scales[:],
                 in_=q_bf[:].rearrange("p q j -> p (q j)"),
             )
-            nc.tensor.matmul_mx(
-                out=scores[c][:],
-                lhsT=q_codes[:].bitcast(FP8X4),
-                lhsT_scale=q_scales[:],
-                rhs=key_words[o][:].bitcast(FP4X4),
-                rhs_scale=key_scales[o],
-                start=(o == 0),
-                stop=(o == PASSES - 1),
-            )
+            w = widths[c]
+            for j, bank in enumerate(scores[c]):
+                nc.tensor.matmul_mx(
+                    out=bank[:],
+                    lhsT=q_codes[:].bitcast(FP8X4),
+                    lhsT_scale=q_scales[:],
+                    rhs=key_words[o][:, 2 * j * w : 2 * (j + 1) * w].bitcast(FP4X4),
+                    rhs_scale=key_scales[o][:, j * w : (j + 1) * w],
+                    start=(o == 0),
+                    stop=(o == PASSES - 1),
+                )
 
         part_words(0, "words0")
         score(0, 0, nc.scalar.copy)
@@ -139,7 +150,12 @@ def tile_attend_rate_topk_kernel(tc, qT, k_words, k_scales, kb, ex, offs, out):
             logit = keep.tile([P, hi - lo], F32, name=f"logit{c}{lo}", align_bytes=64)
             rate = keep.tile([P, hi - lo], F32, name=f"rate{c}{lo}", align_bytes=64)
             result = keep.tile([P, hi - lo], F32, name=f"result{c}{lo}", align_bytes=64)
-            nc.vector.tensor_tensor(out=logit[:], in0=scores[c][:, cols], in1=bias[:, cols], op=ADD)
+            w = widths[c]
+            for a in range(lo, hi, min(w, hi - lo)):
+                b = a + min(w, hi - lo)
+                nc.vector.tensor_tensor(
+                    out=logit[:, a - lo : b - lo], in0=scores[c][a // w][:, a % w : a % w + b - a], in1=bias[:, a:b], op=ADD
+                )
             nc.scalar.activation(out=rate[:], in_=logit[:], func=EXP)
             nc.vector.tensor_scalar_mul(out=result[:], in0=rate[:], scalar1=exposure[:, c : c + 1])
             nc.sync.dma_start(out=out[0, blocks[c], cols], in_=result[:])

@@ -82,12 +82,12 @@ def tile_attend_rate_topk_kernel(tc, qT, k_words, k_scales, kb, ex, offs, out):
             )
         key_scales = [listed_scales[:], pass1_plane[:].bitcast(U8)]
 
-        turned = psum.tile([P, N // P, P], F32, name="turned")
+        turned = psum.tile([P, N // P, P], F32, name="turned", tag="bank12")
         for j in range(N // P):
             nc.tensor.transpose(turned[:, j, :], kb_row[:, j * P : (j + 1) * P], ident[:])
         kb_cols = keep.tile([P, N // P], F32, name="kb_cols", align_bytes=64)
         nc.scalar.copy(out=kb_cols[:], in_=turned[:, :, KB_ROW])
-        spread = psum.tile([P, N], F32, name="spread")
+        spread = psum.tile([P, N], F32, name="spread", tag="bank13")
         for j in range(N // P):
             nc.tensor.transpose(spread[:, j * P : (j + 1) * P], kb_cols[:, j : j + 1].to_broadcast([P, P]), ident[:])
 
@@ -95,10 +95,8 @@ def tile_attend_rate_topk_kernel(tc, qT, k_words, k_scales, kb, ex, offs, out):
         nc.vector.tensor_copy(out=word_pairs[:], in_=word_pool[:].bitcast(U32).indirect(offsets[:]))
         halves = word_pairs[:].bitcast(U16).rearrange("p (i o) -> p o i", o=PASSES)
         blocks = [slice(c * P, (c + 1) * P) for c in range(Q_BLOCKS)]
-        widths = (P, N)
-        scores = [
-            [psum.tile([P, widths[c]], F32, name=f"scores{c}{j}") for j in range(N // widths[c])] for c in range(Q_BLOCKS)
-        ]
+        scores = {}
+        quantised = {}
         key_words = {}
 
         def part_words(o, tag):
@@ -110,7 +108,7 @@ def tile_attend_rate_topk_kernel(tc, qT, k_words, k_scales, kb, ex, offs, out):
             nc.vector.tensor_copy(out=out[:, 0:runs], in_=in_[:, 0:runs])
             nc.scalar.copy(out=out[:, runs : P // LINE], in_=in_[:, runs : P // LINE])
 
-        def score(o, c, copy):
+        def quantise(o, c, copy):
             q_bf = keep.tile([P, P, PACK], BF16, name=f"q_bf{o}{c}", tag=f"rounded{o}{c}", align_bytes=64)
             q_codes = keep.tile([P, P], U32, name=f"q_codes{o}{c}", align_bytes=64)
             q_scales = keep.tile([P, P], U8, name=f"q_scales{o}{c}", align_bytes=64)
@@ -123,10 +121,16 @@ def tile_attend_rate_topk_kernel(tc, qT, k_words, k_scales, kb, ex, offs, out):
                 scales=q_scales[:],
                 in_=q_bf[:].rearrange("p q j -> p (q j)"),
             )
-            w = widths[c]
-            for j, bank in enumerate(scores[c]):
+            quantised[o, c] = (q_codes, q_scales)
+
+        def score(o, c, quarters):
+            q_codes, q_scales = quantised[o, c]
+            w = P
+            for j in quarters:
+                if o == 0:
+                    scores[c, j] = psum.tile([P, P], F32, name=f"scores{c}{j}", tag=f"bank{c}{j}")
                 nc.tensor.matmul_mx(
-                    out=bank[:],
+                    out=scores[c, j][:],
                     lhsT=q_codes[:].bitcast(FP8X4),
                     lhsT_scale=q_scales[:],
                     rhs=key_words[o][:, 2 * j * w : 2 * (j + 1) * w].bitcast(FP4X4),
@@ -136,25 +140,29 @@ def tile_attend_rate_topk_kernel(tc, qT, k_words, k_scales, kb, ex, offs, out):
                 )
 
         part_words(0, "words0")
-        score(0, 0, nc.scalar.copy)
-        score(0, 1, nc.scalar.copy)
+        quantise(0, 0, nc.scalar.copy)
+        score(0, 0, range(4))
+        quantise(0, 1, nc.scalar.copy)
+        score(0, 1, range(3))
         part_words(1, "words1")
-        score(1, 0, shared_copy)
-        score(1, 1, shared_copy)
+        quantise(1, 0, shared_copy)
+        score(1, 0, range(4))
+        quantise(1, 1, shared_copy)
 
         bias = keep.tile([P, N], F32, name="bias", tag="stage1", align_bytes=64)
         nc.scalar.copy(out=bias[:], in_=spread[:])
+        score(1, 1, range(3))
+        score(0, 1, [3])
+        score(1, 1, [3])
 
         for c, lo, hi in PIECES:
             cols = slice(lo, hi)
             logit = keep.tile([P, hi - lo], F32, name=f"logit{c}{lo}", align_bytes=64)
             rate = keep.tile([P, hi - lo], F32, name=f"rate{c}{lo}", align_bytes=64)
             result = keep.tile([P, hi - lo], F32, name=f"result{c}{lo}", align_bytes=64)
-            w = widths[c]
-            for a in range(lo, hi, min(w, hi - lo)):
-                b = a + min(w, hi - lo)
+            for a in range(lo, hi, P):
                 nc.vector.tensor_tensor(
-                    out=logit[:, a - lo : b - lo], in0=scores[c][a // w][:, a % w : a % w + b - a], in1=bias[:, a:b], op=ADD
+                    out=logit[:, a - lo : a - lo + P], in0=scores[c, a // P][:], in1=bias[:, a : a + P], op=ADD
                 )
             nc.scalar.activation(out=rate[:], in_=logit[:], func=EXP)
             nc.vector.tensor_scalar_mul(out=result[:], in0=rate[:], scalar1=exposure[:, c : c + 1])

@@ -17,19 +17,22 @@ FP8X4 = mybir.dt.float8_e4m3fn_x4
 FP4X4 = mybir.dt.float4_e2m1fn_x4
 EXP = mybir.ActivationFunctionType.Exp
 ADD = mybir.AluOpType.add
+MULT = mybir.AluOpType.mult
 
 P = 128
 PACK = 4
 K_PASS = P * PACK
 PASSES = D // K_PASS
 Q_BLOCKS = NQ // P
+QUARTERS = N // P
 QUADRANT = 32
 GROUP = 4
 SPARE_ROW = GROUP
 KB_ROW = P - 1
-VECTOR_SHARE = 64
 LINE = 4
+VECTOR_SHARE = 80
 PIECES = ((0, 0, 128), (0, 128, 256), (0, 256, 512), (1, 0, 256), (1, 256, 384), (1, 384, 512))
+GPSIMD_PIECES = 2
 
 
 def tile_attend_rate_topk_kernel(tc, qT, k_words, k_scales, kb, ex, offs, out):
@@ -42,7 +45,9 @@ def tile_attend_rate_topk_kernel(tc, qT, k_words, k_scales, kb, ex, offs, out):
         scale_pool = keep.tile([P, T // 4], I32, name="scale_pool", align_bytes=64)
         kb_pool = keep.tile([P, T], F32, name="kb_pool", align_bytes=64)
         word_pool = keep.tile([P, T], I32, name="word_pool", align_bytes=64)
-        q_raw = [keep.tile([P, PACK, NQ], F32, name=f"q_raw{o}", tag=f"stage{o}", align_bytes=64) for o in range(PASSES)]
+        q_raw = [
+            keep.tile([P, PACK, NQ], F32, name=f"q_raw{o}", tag=f"stage{o}", align_bytes=64) for o in range(PASSES)
+        ]
         exposure = keep.tile([P, Q_BLOCKS], F32, name="exposure")
         ident = keep.tile([P, P], F32, name="ident", align_bytes=64)
         warm_in = keep.tile([P, 1], F32, name="warm_in")
@@ -82,13 +87,13 @@ def tile_attend_rate_topk_kernel(tc, qT, k_words, k_scales, kb, ex, offs, out):
             )
         key_scales = [listed_scales[:], pass1_plane[:].bitcast(U8)]
 
-        turned = psum.tile([P, N // P, P], F32, name="turned", tag="bank12")
-        for j in range(N // P):
+        turned = psum.tile([P, QUARTERS, P], F32, name="turned", tag="bank12")
+        for j in range(QUARTERS):
             nc.tensor.transpose(turned[:, j, :], kb_row[:, j * P : (j + 1) * P], ident[:])
-        kb_cols = keep.tile([P, N // P], F32, name="kb_cols", align_bytes=64)
+        kb_cols = keep.tile([P, QUARTERS], F32, name="kb_cols", align_bytes=64)
         nc.scalar.copy(out=kb_cols[:], in_=turned[:, :, KB_ROW])
         spread = psum.tile([P, N], F32, name="spread", tag="bank13")
-        for j in range(N // P):
+        for j in range(QUARTERS):
             nc.tensor.transpose(spread[:, j * P : (j + 1) * P], kb_cols[:, j : j + 1].to_broadcast([P, P]), ident[:])
 
         word_pairs = keep.tile([P, N], U32, name="word_pairs", align_bytes=64)
@@ -99,8 +104,8 @@ def tile_attend_rate_topk_kernel(tc, qT, k_words, k_scales, kb, ex, offs, out):
         quantised = {}
         key_words = {}
 
-        def part_words(o, tag):
-            key_words[o] = keep.tile([P, 2 * N], U8, name=f"key_words{o}", tag=tag, align_bytes=64)
+        def part_words(o):
+            key_words[o] = keep.tile([P, 2 * N], U8, name=f"key_words{o}", align_bytes=64)
             nc.vector.tensor_copy(out=key_words[o][:].bitcast(U16), in_=halves[:, o, :])
 
         def shared_copy(out, in_):
@@ -109,7 +114,7 @@ def tile_attend_rate_topk_kernel(tc, qT, k_words, k_scales, kb, ex, offs, out):
             nc.scalar.copy(out=out[:, runs : P // LINE], in_=in_[:, runs : P // LINE])
 
         def quantise(o, c, copy):
-            q_bf = keep.tile([P, P, PACK], BF16, name=f"q_bf{o}{c}", tag=f"rounded{o}{c}", align_bytes=64)
+            q_bf = keep.tile([P, P, PACK], BF16, name=f"q_bf{o}{c}", align_bytes=64)
             q_codes = keep.tile([P, P], U32, name=f"q_codes{o}{c}", align_bytes=64)
             q_scales = keep.tile([P, P], U8, name=f"q_scales{o}{c}", align_bytes=64)
             copy(
@@ -125,7 +130,6 @@ def tile_attend_rate_topk_kernel(tc, qT, k_words, k_scales, kb, ex, offs, out):
 
         def score(o, c, quarters):
             q_codes, q_scales = quantised[o, c]
-            w = P
             for j in quarters:
                 if o == 0:
                     scores[c, j] = psum.tile([P, P], F32, name=f"scores{c}{j}", tag=f"bank{c}{j}")
@@ -133,29 +137,30 @@ def tile_attend_rate_topk_kernel(tc, qT, k_words, k_scales, kb, ex, offs, out):
                     out=scores[c, j][:],
                     lhsT=q_codes[:].bitcast(FP8X4),
                     lhsT_scale=q_scales[:],
-                    rhs=key_words[o][:, 2 * j * w : 2 * (j + 1) * w].bitcast(FP4X4),
-                    rhs_scale=key_scales[o][:, j * w : (j + 1) * w],
+                    rhs=key_words[o][:, 2 * j * P : 2 * (j + 1) * P].bitcast(FP4X4),
+                    rhs_scale=key_scales[o][:, j * P : (j + 1) * P],
                     start=(o == 0),
                     stop=(o == PASSES - 1),
                 )
 
-        part_words(0, "words0")
+        every, last = range(QUARTERS), QUARTERS - 1
+        part_words(0)
         quantise(0, 0, nc.scalar.copy)
-        score(0, 0, range(4))
+        score(0, 0, every)
         quantise(0, 1, nc.scalar.copy)
-        score(0, 1, range(3))
-        part_words(1, "words1")
+        score(0, 1, every[:last])
+        part_words(1)
         quantise(1, 0, shared_copy)
-        score(1, 0, range(4))
+        score(1, 0, every)
         quantise(1, 1, shared_copy)
 
         bias = keep.tile([P, N], F32, name="bias", tag="stage1", align_bytes=64)
         nc.scalar.copy(out=bias[:], in_=spread[:])
-        score(1, 1, range(3))
-        score(0, 1, [3])
-        score(1, 1, [3])
+        score(1, 1, every[:last])
+        score(0, 1, every[last:])
+        score(1, 1, every[last:])
 
-        for c, lo, hi in PIECES:
+        for piece, (c, lo, hi) in enumerate(PIECES):
             cols = slice(lo, hi)
             logit = keep.tile([P, hi - lo], F32, name=f"logit{c}{lo}", align_bytes=64)
             rate = keep.tile([P, hi - lo], F32, name=f"rate{c}{lo}", align_bytes=64)
@@ -165,5 +170,10 @@ def tile_attend_rate_topk_kernel(tc, qT, k_words, k_scales, kb, ex, offs, out):
                     out=logit[:, a - lo : a - lo + P], in0=scores[c, a // P][:], in1=bias[:, a : a + P], op=ADD
                 )
             nc.scalar.activation(out=rate[:], in_=logit[:], func=EXP)
-            nc.vector.tensor_scalar_mul(out=result[:], in0=rate[:], scalar1=exposure[:, c : c + 1])
+            if piece < GPSIMD_PIECES:
+                nc.gpsimd.tensor_scalar(
+                    out=result[:], in0=rate[:], scalar1=exposure[:, c : c + 1], scalar2=0.0, op0=MULT, op1=ADD
+                )
+            else:
+                nc.vector.tensor_scalar_mul(out=result[:], in0=rate[:], scalar1=exposure[:, c : c + 1])
             nc.sync.dma_start(out=out[0, blocks[c], cols], in_=result[:])

@@ -25,14 +25,16 @@ K_PASS = P * PACK
 PASSES = D // K_PASS
 Q_BLOCKS = NQ // P
 QUARTERS = N // P
+HALF = N // 2
+WORDS_FIRST = 1280
 QUADRANT = 32
 GROUP = 4
 SPARE_ROW = GROUP
 KB_ROW = P - 1
 LINE = 4
 VECTOR_SHARE = 80
-PIECES = ((0, 0, 128), (0, 128, 256), (0, 256, 512), (1, 0, 256), (1, 256, 384), (1, 384, 512))
-GPSIMD_PIECES = 2
+PIECES = ((0, 0, 256), (0, 256, 512), (1, 0, 256), (1, 256, 384), (1, 384, 512))
+GPSIMD_PIECES = 0
 
 
 def tile_attend_rate_topk_kernel(tc, qT, k_words, k_scales, kb, ex, offs, out):
@@ -42,13 +44,12 @@ def tile_attend_rate_topk_kernel(tc, qT, k_words, k_scales, kb, ex, offs, out):
         psum = ctx.enter_context(tc.psum_pool(name="psum", bufs=1))
 
         offsets = keep.tile([P, N // 16], U16, name="offsets")
-        scale_pool = keep.tile([P, T // 4], I32, name="scale_pool", align_bytes=64)
+        scale_pool = keep.tile([P, T // 4], I32, name="scale_pool", tag="scale_pool", align_bytes=64)
         kb_pool = keep.tile([P, T], F32, name="kb_pool", align_bytes=64)
         word_pool = keep.tile([P, T], I32, name="word_pool", align_bytes=64)
         q_raw = [
             keep.tile([P, PACK, NQ], F32, name=f"q_raw{o}", tag=f"stage{o}", align_bytes=64) for o in range(PASSES)
         ]
-        exposure = keep.tile([P, Q_BLOCKS], F32, name="exposure")
         ident = keep.tile([P, P], F32, name="ident", align_bytes=64)
         warm_in = keep.tile([P, 1], F32, name="warm_in")
         warm_out = keep.tile([P, 1], F32, name="warm_out")
@@ -57,56 +58,70 @@ def tile_attend_rate_topk_kernel(tc, qT, k_words, k_scales, kb, ex, offs, out):
         nc.gpsimd.memset(scale_pool[:], 0)
         nc.gpsimd.memset(warm_in[:], 0.0)
         make_identity(nc, ident[:])
+        nc.gpsimd.memset(pass1_plane[:], 0)
         nc.vector.memset(kb_pool[0:KB_ROW, :], 0.0)
-        nc.vector.memset(pass1_plane[:], 0)
 
-        nc.sync.dma_start(out=kb_pool[KB_ROW:P, :], in_=kb[0:1, :])
         nc.sync.dma_start(offsets[:], offs)
+        nc.sync.dma_start(out=kb_pool[KB_ROW:P, :], in_=kb[0:1, :])
+        words = k_words[0].rearrange("p t b -> p (t b)").bitcast(I32)
+        nc.sync.dma_start(out=word_pool[:, 0:WORDS_FIRST], in_=words[:, 0:WORDS_FIRST])
         scale_rows = k_scales.bitcast(I32)
-        nc.scalar.dma_start(out=scale_pool[SPARE_ROW : SPARE_ROW + GROUP * GROUP, :], in_=scale_rows[1])
         for r in range(GROUP):
             nc.sync.dma_start(out=scale_pool[r:P:QUADRANT, :], in_=scale_rows[0, r : GROUP * GROUP : GROUP, :])
+        nc.sync.dma_start(out=scale_pool[SPARE_ROW : SPARE_ROW + GROUP * GROUP, :], in_=scale_rows[1])
         nc.scalar.activation(out=warm_out[:], in_=warm_in[:], func=EXP)
-        nc.sync.dma_start(out=word_pool[:], in_=k_words[0].rearrange("p t b -> p (t b)").bitcast(I32))
+        nc.sync.dma_start(out=word_pool[:, WORDS_FIRST:T], in_=words[:, WORDS_FIRST:T])
         for o in range(PASSES):
             rows = qT[0, o * K_PASS : (o + 1) * K_PASS, :]
             nc.sync.dma_start(out=q_raw[o][:], in_=rows.rearrange("(p j) q -> p j q", j=PACK))
-        with nc.allow_non_contiguous_dma(reason="one exposure a query row"):
-            nc.sync.dma_start(out=exposure[:], in_=ex[0].rearrange("(c p) one -> p (c one)", p=P))
 
-        kb_row = keep.tile([P, N], F32, name="kb_row", align_bytes=64)
-        nc.vector.tensor_copy(out=kb_row[:], in_=kb_pool[:].indirect(offsets[:]))
+        kb_row = [keep.tile([P, HALF], F32, name=f"kb_row{h}", tag=f"row{h}", align_bytes=64) for h in range(2)]
+        for h in range(2):
+            entries = offsets[:, h * HALF // 16 : (h + 1) * HALF // 16]
+            nc.vector.tensor_copy(out=kb_row[h][:], in_=kb_pool[:].indirect(entries))
 
         listed_scales = keep.tile([P, N], U8, name="listed_scales", align_bytes=64)
         nc.vector.tensor_copy(out=listed_scales[:], in_=scale_pool[:].bitcast(U8).indirect(offsets[:]))
+
+        kb_cols = []
+        for h in range(2):
+            turned = psum.tile([P, 2, P], F32, name=f"turned{h}", tag=f"bank1{h}")
+            for j in range(2):
+                nc.tensor.transpose(turned[:, j, :], kb_row[h][:, j * P : (j + 1) * P], ident[:])
+            kb_cols.append(keep.tile([P, 2], F32, name=f"kb_cols{h}", align_bytes=64))
+            nc.scalar.copy(out=kb_cols[h][:], in_=turned[:, :, KB_ROW])
         for g in range(GROUP):
             first = SPARE_ROW + GROUP * g
-            nc.scalar.dma_start(
+            nc.sync.dma_start(
                 out=pass1_plane[QUADRANT * g : QUADRANT * g + GROUP, :],
                 in_=listed_scales[first : first + GROUP, :].bitcast(I32),
             )
         key_scales = [listed_scales[:], pass1_plane[:].bitcast(U8)]
-
-        turned = psum.tile([P, QUARTERS, P], F32, name="turned", tag="bank12")
-        for j in range(QUARTERS):
-            nc.tensor.transpose(turned[:, j, :], kb_row[:, j * P : (j + 1) * P], ident[:])
-        kb_cols = keep.tile([P, QUARTERS], F32, name="kb_cols", align_bytes=64)
-        nc.scalar.copy(out=kb_cols[:], in_=turned[:, :, KB_ROW])
+        exposure = keep.tile([P, Q_BLOCKS], F32, name="exposure", tag="scale_pool", align_bytes=64)
+        with nc.allow_non_contiguous_dma(reason="one exposure a query row"):
+            nc.sync.dma_start(out=exposure[:], in_=ex[0].rearrange("(c p) one -> p (c one)", p=P))
         spread = psum.tile([P, N], F32, name="spread", tag="bank13")
         for j in range(QUARTERS):
-            nc.tensor.transpose(spread[:, j * P : (j + 1) * P], kb_cols[:, j : j + 1].to_broadcast([P, P]), ident[:])
+            column = kb_cols[j // 2][:, j % 2 : j % 2 + 1]
+            nc.tensor.transpose(spread[:, j * P : (j + 1) * P], column.to_broadcast([P, P]), ident[:])
 
         word_pairs = keep.tile([P, N], U32, name="word_pairs", align_bytes=64)
-        nc.vector.tensor_copy(out=word_pairs[:], in_=word_pool[:].bitcast(U32).indirect(offsets[:]))
+        for h in range(2):
+            entries = offsets[:, h * HALF // 16 : (h + 1) * HALF // 16]
+            nc.vector.tensor_copy(
+                out=word_pairs[:, h * HALF : (h + 1) * HALF], in_=word_pool[:].bitcast(U32).indirect(entries)
+            )
         halves = word_pairs[:].bitcast(U16).rearrange("p (i o) -> p o i", o=PASSES)
         blocks = [slice(c * P, (c + 1) * P) for c in range(Q_BLOCKS)]
         scores = {}
         quantised = {}
         key_words = {}
 
-        def part_words(o):
-            key_words[o] = keep.tile([P, 2 * N], U8, name=f"key_words{o}", align_bytes=64)
-            nc.vector.tensor_copy(out=key_words[o][:].bitcast(U16), in_=halves[:, o, :])
+        def part_words(o, pieces):
+            key_words[o] = keep.tile([P, 2 * N], U8, name=f"key_words{o}", tag=("words0", "rounded1")[o], align_bytes=64)
+            for a in range(0, N, N // pieces):
+                cols = slice(a, a + N // pieces)
+                nc.vector.tensor_copy(out=key_words[o][:].bitcast(U16)[:, cols], in_=halves[:, o, cols])
 
         def shared_copy(out, in_):
             runs = VECTOR_SHARE // LINE
@@ -114,7 +129,7 @@ def tile_attend_rate_topk_kernel(tc, qT, k_words, k_scales, kb, ex, offs, out):
             nc.scalar.copy(out=out[:, runs : P // LINE], in_=in_[:, runs : P // LINE])
 
         def quantise(o, c, copy):
-            q_bf = keep.tile([P, P, PACK], BF16, name=f"q_bf{o}{c}", align_bytes=64)
+            q_bf = keep.tile([P, P, PACK], BF16, name=f"q_bf{o}{c}", tag=f"rounded{c * (1 + o)}", align_bytes=64)
             q_codes = keep.tile([P, P], U32, name=f"q_codes{o}{c}", align_bytes=64)
             q_scales = keep.tile([P, P], U8, name=f"q_scales{o}{c}", align_bytes=64)
             copy(
@@ -143,22 +158,20 @@ def tile_attend_rate_topk_kernel(tc, qT, k_words, k_scales, kb, ex, offs, out):
                     stop=(o == PASSES - 1),
                 )
 
-        every, last = range(QUARTERS), QUARTERS - 1
-        part_words(0)
+        every = range(QUARTERS)
+        part_words(0, 2)
         quantise(0, 0, nc.scalar.copy)
         score(0, 0, every)
         quantise(0, 1, nc.scalar.copy)
-        score(0, 1, every[:last])
-        part_words(1)
-        quantise(1, 0, shared_copy)
-        score(1, 0, every)
-        quantise(1, 1, shared_copy)
-
-        bias = keep.tile([P, N], F32, name="bias", tag="stage1", align_bytes=64)
+        bias = keep.tile([P, N], F32, name="bias", tag="stage0", align_bytes=64)
         nc.scalar.copy(out=bias[:], in_=spread[:])
-        score(1, 1, every[:last])
-        score(0, 1, every[last:])
-        score(1, 1, every[last:])
+        score(0, 1, every)
+        part_words(1, 1)
+        quantise(1, 0, nc.vector.tensor_copy)
+        score(1, 0, every)
+        quantise(1, 1, nc.scalar.copy)
+
+        score(1, 1, every)
 
         for piece, (c, lo, hi) in enumerate(PIECES):
             cols = slice(lo, hi)
@@ -169,7 +182,7 @@ def tile_attend_rate_topk_kernel(tc, qT, k_words, k_scales, kb, ex, offs, out):
                 nc.vector.tensor_tensor(
                     out=logit[:, a - lo : a - lo + P], in0=scores[c, a // P][:], in1=bias[:, a : a + P], op=ADD
                 )
-            nc.scalar.activation(out=rate[:], in_=logit[:], func=EXP)
+                nc.scalar.activation(out=rate[:, a - lo : a - lo + P], in_=logit[:, a - lo : a - lo + P], func=EXP)
             if piece < GPSIMD_PIECES:
                 nc.gpsimd.tensor_scalar(
                     out=result[:], in0=rate[:], scalar1=exposure[:, c : c + 1], scalar2=0.0, op0=MULT, op1=ADD

@@ -41,6 +41,7 @@ def tile_attend_rate_topk_kernel(tc, qT, k_words, k_scales, kb, ex, offs, out):
     nc = tc.nc
     with ExitStack() as ctx:
         keep = ctx.enter_context(tc.tile_pool(name="keep", bufs=1))
+        stage = ctx.enter_context(tc.tile_pool(name="stage", bufs=1))
         psum = ctx.enter_context(tc.psum_pool(name="psum", bufs=1))
 
         offsets = keep.tile([P, N // 16], U16, name="offsets")
@@ -48,7 +49,8 @@ def tile_attend_rate_topk_kernel(tc, qT, k_words, k_scales, kb, ex, offs, out):
         kb_pool = keep.tile([P, T], F32, name="kb_pool", align_bytes=64)
         word_pool = keep.tile([P, T], I32, name="word_pool", align_bytes=64)
         q_raw = [
-            keep.tile([P, PACK, NQ], F32, name=f"q_raw{o}", tag=f"stage{o}", align_bytes=64) for o in range(PASSES)
+            stage.tile([P, PACK, NQ], F32, name=f"q_raw{o}", offset=o * 4 * PACK * NQ, align_bytes=64)
+            for o in range(PASSES)
         ]
         ident = keep.tile([P, P], F32, name="ident", align_bytes=64)
         warm_in = keep.tile([P, 1], F32, name="warm_in")
@@ -100,10 +102,15 @@ def tile_attend_rate_topk_kernel(tc, qT, k_words, k_scales, kb, ex, offs, out):
         exposure = keep.tile([P, Q_BLOCKS], F32, name="exposure", tag="scale_pool", align_bytes=64)
         with nc.allow_non_contiguous_dma(reason="one exposure a query row"):
             nc.sync.dma_start(out=exposure[:], in_=ex[0].rearrange("(c p) one -> p (c one)", p=P))
-        spread = psum.tile([P, N], F32, name="spread", tag="bank13")
-        for j in range(QUARTERS):
-            column = kb_cols[j // 2][:, j % 2 : j % 2 + 1]
-            nc.tensor.transpose(spread[:, j * P : (j + 1) * P], column.to_broadcast([P, P]), ident[:])
+        spread = []
+        for h in range(2):
+            spread.append(psum.tile([P, HALF], F32, name=f"spread{h}", tag=f"bank1{2 + h}"))
+            for j in range(2):
+                nc.tensor.transpose(
+                    spread[h][:, j * P : (j + 1) * P], kb_cols[h][:, j : j + 1].to_broadcast([P, P]), ident[:]
+                )
+        bias = [keep.tile([P, HALF], F32, name="bias0", align_bytes=64)]
+        nc.scalar.copy(out=bias[0][:], in_=spread[0][:])
 
         word_pairs = keep.tile([P, N], U32, name="word_pairs", align_bytes=64)
         for h in range(2):
@@ -117,11 +124,9 @@ def tile_attend_rate_topk_kernel(tc, qT, k_words, k_scales, kb, ex, offs, out):
         quantised = {}
         key_words = {}
 
-        def part_words(o, pieces):
-            key_words[o] = keep.tile([P, 2 * N], U8, name=f"key_words{o}", tag=("words0", "rounded1")[o], align_bytes=64)
-            for a in range(0, N, N // pieces):
-                cols = slice(a, a + N // pieces)
-                nc.vector.tensor_copy(out=key_words[o][:].bitcast(U16)[:, cols], in_=halves[:, o, cols])
+        def part_words(o, h, tag):
+            key_words[o, h] = keep.tile([P, 2 * HALF], U8, name=f"key_words{o}{h}", tag=tag, align_bytes=64)
+            nc.vector.tensor_copy(out=key_words[o, h][:].bitcast(U16), in_=halves[:, o, h * HALF : (h + 1) * HALF])
 
         def shared_copy(out, in_):
             runs = VECTOR_SHARE // LINE
@@ -129,7 +134,10 @@ def tile_attend_rate_topk_kernel(tc, qT, k_words, k_scales, kb, ex, offs, out):
             nc.scalar.copy(out=out[:, runs : P // LINE], in_=in_[:, runs : P // LINE])
 
         def quantise(o, c, copy):
-            q_bf = keep.tile([P, P, PACK], BF16, name=f"q_bf{o}{c}", tag=f"rounded{c * (1 + o)}", align_bytes=64)
+            if (o, c) == (1, 1):
+                q_bf = stage.tile([P, P, PACK], BF16, name="q_bf11", offset=4 * N, align_bytes=64)
+            else:
+                q_bf = keep.tile([P, P, PACK], BF16, name=f"q_bf{o}{c}", tag=f"rounded{c + 2 * o}", align_bytes=64)
             q_codes = keep.tile([P, P], U32, name=f"q_codes{o}{c}", align_bytes=64)
             q_scales = keep.tile([P, P], U8, name=f"q_scales{o}{c}", align_bytes=64)
             copy(
@@ -152,22 +160,24 @@ def tile_attend_rate_topk_kernel(tc, qT, k_words, k_scales, kb, ex, offs, out):
                     out=scores[c, j][:],
                     lhsT=q_codes[:].bitcast(FP8X4),
                     lhsT_scale=q_scales[:],
-                    rhs=key_words[o][:, 2 * j * P : 2 * (j + 1) * P].bitcast(FP4X4),
+                    rhs=key_words[o, j // 2][:, 2 * (j % 2) * P : 2 * (j % 2 + 1) * P].bitcast(FP4X4),
                     rhs_scale=key_scales[o][:, j * P : (j + 1) * P],
                     start=(o == 0),
                     stop=(o == PASSES - 1),
                 )
 
         every = range(QUARTERS)
-        part_words(0, 2)
+        part_words(0, 0, "words00")
         quantise(0, 0, nc.scalar.copy)
+        part_words(0, 1, "rounded0")
         score(0, 0, every)
         quantise(0, 1, nc.scalar.copy)
-        bias = keep.tile([P, N], F32, name="bias", tag="stage0", align_bytes=64)
-        nc.scalar.copy(out=bias[:], in_=spread[:])
+        bias.append(stage.tile([P, HALF], F32, name="bias1", offset=0, align_bytes=64))
+        nc.scalar.copy(out=bias[1][:], in_=spread[1][:])
         score(0, 1, every)
-        part_words(1, 1)
+        part_words(1, 0, "rounded1")
         quantise(1, 0, nc.vector.tensor_copy)
+        part_words(1, 1, "rounded2")
         score(1, 0, every)
         quantise(1, 1, nc.scalar.copy)
 
@@ -180,7 +190,7 @@ def tile_attend_rate_topk_kernel(tc, qT, k_words, k_scales, kb, ex, offs, out):
             result = keep.tile([P, hi - lo], F32, name=f"result{c}{lo}", align_bytes=64)
             for a in range(lo, hi, P):
                 nc.vector.tensor_tensor(
-                    out=logit[:, a - lo : a - lo + P], in0=scores[c, a // P][:], in1=bias[:, a : a + P], op=ADD
+                    out=logit[:, a - lo : a - lo + P], in0=scores[c, a // P][:], in1=bias[a // HALF][:, a % HALF : a % HALF + P], op=ADD
                 )
                 nc.scalar.activation(out=rate[:, a - lo : a - lo + P], in_=logit[:, a - lo : a - lo + P], func=EXP)
             if piece < GPSIMD_PIECES:

@@ -26,7 +26,7 @@ PASSES = D // K_PASS
 Q_BLOCKS = NQ // P
 QUARTERS = N // P
 HALF = N // 2
-WORDS_FIRST = 1280
+WORDS_FIRST = 896
 QUADRANT = 32
 GROUP = 4
 SPARE_ROW = GROUP

@@ -17,7 +17,6 @@ FP8X4 = mybir.dt.float8_e4m3fn_x4
 FP4X4 = mybir.dt.float4_e2m1fn_x4
 EXP = mybir.ActivationFunctionType.Exp
 ADD = mybir.AluOpType.add
-MULT = mybir.AluOpType.mult
 
 P = 128
 PACK = 4
@@ -25,32 +24,33 @@ K_PASS = P * PACK
 PASSES = D // K_PASS
 Q_BLOCKS = NQ // P
 QUARTERS = N // P
-HALF = N // 2
-WORDS_FIRST = 896
+HALVES = 2
+HALF = N // HALVES
+LIST_GROUP = 16
 QUADRANT = 32
 GROUP = 4
 SPARE_ROW = GROUP
 KB_ROW = P - 1
 LINE = 4
-VECTOR_SHARE = 80
+WORDS_FIRST = 896
+SCORE_BANKS = ((0, 1, 2, 3), (4, 5, 6, 0))
+TURN_BANKS = (4, 5)
+SPREAD_BANKS = (6, 7)
 PIECES = ((0, 0, 256), (0, 256, 512), (1, 0, 256), (1, 256, 384), (1, 384, 512))
-GPSIMD_PIECES = 0
 
 
 def tile_attend_rate_topk_kernel(tc, qT, k_words, k_scales, kb, ex, offs, out):
     nc = tc.nc
     with ExitStack() as ctx:
         keep = ctx.enter_context(tc.tile_pool(name="keep", bufs=1))
-        stage = ctx.enter_context(tc.tile_pool(name="stage", bufs=1))
         psum = ctx.enter_context(tc.psum_pool(name="psum", bufs=1))
 
-        offsets = keep.tile([P, N // 16], U16, name="offsets")
+        offsets = keep.tile([P, N // LIST_GROUP], U16, name="offsets")
         scale_pool = keep.tile([P, T // 4], I32, name="scale_pool", tag="scale_pool", align_bytes=64)
         kb_pool = keep.tile([P, T], F32, name="kb_pool", align_bytes=64)
         word_pool = keep.tile([P, T], I32, name="word_pool", align_bytes=64)
         q_raw = [
-            stage.tile([P, PACK, NQ], F32, name=f"q_raw{o}", offset=o * 4 * PACK * NQ, align_bytes=64)
-            for o in range(PASSES)
+            keep.tile([P, PACK, NQ], F32, name=f"q_raw{o}", tag=f"raw{o}", align_bytes=64) for o in range(PASSES)
         ]
         ident = keep.tile([P, P], F32, name="ident", align_bytes=64)
         warm_in = keep.tile([P, 1], F32, name="warm_in")
@@ -77,21 +77,25 @@ def tile_attend_rate_topk_kernel(tc, qT, k_words, k_scales, kb, ex, offs, out):
             rows = qT[0, o * K_PASS : (o + 1) * K_PASS, :]
             nc.sync.dma_start(out=q_raw[o][:], in_=rows.rearrange("(p j) q -> p j q", j=PACK))
 
-        kb_row = [keep.tile([P, HALF], F32, name=f"kb_row{h}", tag=f"row{h}", align_bytes=64) for h in range(2)]
-        for h in range(2):
-            entries = offsets[:, h * HALF // 16 : (h + 1) * HALF // 16]
-            nc.vector.tensor_copy(out=kb_row[h][:], in_=kb_pool[:].indirect(entries))
+        entries = [offsets[:, h * HALF // LIST_GROUP : (h + 1) * HALF // LIST_GROUP] for h in range(HALVES)]
+        slots = [slice(h * HALF, (h + 1) * HALF) for h in range(HALVES)]
+
+        kb_row = [keep.tile([P, HALF], F32, name=f"kb_row{h}", align_bytes=64) for h in range(HALVES)]
+        for h in range(HALVES):
+            nc.vector.tensor_copy(out=kb_row[h][:], in_=kb_pool[:].indirect(entries[h]))
 
         listed_scales = keep.tile([P, N], U8, name="listed_scales", align_bytes=64)
         nc.vector.tensor_copy(out=listed_scales[:], in_=scale_pool[:].bitcast(U8).indirect(offsets[:]))
 
+        per_half = QUARTERS // HALVES
         kb_cols = []
-        for h in range(2):
-            turned = psum.tile([P, 2, P], F32, name=f"turned{h}", tag=f"bank1{h}")
-            for j in range(2):
+        for h in range(HALVES):
+            turned = psum.tile([P, per_half, P], F32, name=f"turned{h}", tag=f"bank{TURN_BANKS[h]}")
+            for j in range(per_half):
                 nc.tensor.transpose(turned[:, j, :], kb_row[h][:, j * P : (j + 1) * P], ident[:])
-            kb_cols.append(keep.tile([P, 2], F32, name=f"kb_cols{h}", align_bytes=64))
+            kb_cols.append(keep.tile([P, per_half], F32, name=f"kb_cols{h}", align_bytes=64))
             nc.scalar.copy(out=kb_cols[h][:], in_=turned[:, :, KB_ROW])
+
         for g in range(GROUP):
             first = SPARE_ROW + GROUP * g
             nc.sync.dma_start(
@@ -99,45 +103,44 @@ def tile_attend_rate_topk_kernel(tc, qT, k_words, k_scales, kb, ex, offs, out):
                 in_=listed_scales[first : first + GROUP, :].bitcast(I32),
             )
         key_scales = [listed_scales[:], pass1_plane[:].bitcast(U8)]
+
         exposure = keep.tile([P, Q_BLOCKS], F32, name="exposure", tag="scale_pool", align_bytes=64)
         with nc.allow_non_contiguous_dma(reason="one exposure a query row"):
             nc.sync.dma_start(out=exposure[:], in_=ex[0].rearrange("(c p) one -> p (c one)", p=P))
+
         spread = []
-        for h in range(2):
-            spread.append(psum.tile([P, HALF], F32, name=f"spread{h}", tag=f"bank1{2 + h}"))
-            for j in range(2):
+        for h in range(HALVES):
+            spread.append(psum.tile([P, HALF], F32, name=f"spread{h}", tag=f"bank{SPREAD_BANKS[h]}"))
+            for j in range(per_half):
                 nc.tensor.transpose(
                     spread[h][:, j * P : (j + 1) * P], kb_cols[h][:, j : j + 1].to_broadcast([P, P]), ident[:]
                 )
-        bias = [keep.tile([P, HALF], F32, name="bias0", align_bytes=64)]
-        nc.scalar.copy(out=bias[0][:], in_=spread[0][:])
+
+        bias = {}
+
+        def copy_bias(h, tag):
+            bias[h] = keep.tile([P, HALF], F32, name=f"bias{h}", tag=tag, align_bytes=64)
+            nc.scalar.copy(out=bias[h][:], in_=spread[h][:])
+
+        copy_bias(0, "bias0")
 
         word_pairs = keep.tile([P, N], U32, name="word_pairs", align_bytes=64)
-        for h in range(2):
-            entries = offsets[:, h * HALF // 16 : (h + 1) * HALF // 16]
-            nc.vector.tensor_copy(
-                out=word_pairs[:, h * HALF : (h + 1) * HALF], in_=word_pool[:].bitcast(U32).indirect(entries)
-            )
-        halves = word_pairs[:].bitcast(U16).rearrange("p (i o) -> p o i", o=PASSES)
+        for h in range(HALVES):
+            nc.vector.tensor_copy(out=word_pairs[:, slots[h]], in_=word_pool[:].bitcast(U32).indirect(entries[h]))
+
+        by_pass = word_pairs[:].bitcast(U16).rearrange("p (i o) -> p o i", o=PASSES)
+        key_words = {}
+        for o in range(PASSES):
+            for h in range(HALVES):
+                key_words[o, h] = keep.tile([P, 2 * HALF], U8, name=f"key_words{o}{h}", align_bytes=64)
+                nc.vector.tensor_copy(out=key_words[o, h][:].bitcast(U16), in_=by_pass[:, o, slots[h]])
+
         blocks = [slice(c * P, (c + 1) * P) for c in range(Q_BLOCKS)]
         scores = {}
         quantised = {}
-        key_words = {}
 
-        def part_words(o, h, tag):
-            key_words[o, h] = keep.tile([P, 2 * HALF], U8, name=f"key_words{o}{h}", tag=tag, align_bytes=64)
-            nc.vector.tensor_copy(out=key_words[o, h][:].bitcast(U16), in_=halves[:, o, h * HALF : (h + 1) * HALF])
-
-        def shared_copy(out, in_):
-            runs = VECTOR_SHARE // LINE
-            nc.vector.tensor_copy(out=out[:, 0:runs], in_=in_[:, 0:runs])
-            nc.scalar.copy(out=out[:, runs : P // LINE], in_=in_[:, runs : P // LINE])
-
-        def quantise(o, c, copy):
-            if (o, c) == (1, 1):
-                q_bf = stage.tile([P, P, PACK], BF16, name="q_bf11", offset=4 * N, align_bytes=64)
-            else:
-                q_bf = keep.tile([P, P, PACK], BF16, name=f"q_bf{o}{c}", tag=f"rounded{c + 2 * o}", align_bytes=64)
+        def quantise(o, c, copy, tag):
+            q_bf = keep.tile([P, P, PACK], BF16, name=f"q_bf{o}{c}", tag=tag, align_bytes=64)
             q_codes = keep.tile([P, P], U32, name=f"q_codes{o}{c}", align_bytes=64)
             q_scales = keep.tile([P, P], U8, name=f"q_scales{o}{c}", align_bytes=64)
             copy(
@@ -155,48 +158,42 @@ def tile_attend_rate_topk_kernel(tc, qT, k_words, k_scales, kb, ex, offs, out):
             q_codes, q_scales = quantised[o, c]
             for j in quarters:
                 if o == 0:
-                    scores[c, j] = psum.tile([P, P], F32, name=f"scores{c}{j}", tag=f"bank{c}{j}")
+                    scores[c, j] = psum.tile([P, P], F32, name=f"scores{c}{j}", tag=f"bank{SCORE_BANKS[c][j]}")
+                h, inside = divmod(j, per_half)
                 nc.tensor.matmul_mx(
                     out=scores[c, j][:],
                     lhsT=q_codes[:].bitcast(FP8X4),
                     lhsT_scale=q_scales[:],
-                    rhs=key_words[o, j // 2][:, 2 * (j % 2) * P : 2 * (j % 2 + 1) * P].bitcast(FP4X4),
+                    rhs=key_words[o, h][:, 2 * inside * P : 2 * (inside + 1) * P].bitcast(FP4X4),
                     rhs_scale=key_scales[o][:, j * P : (j + 1) * P],
                     start=(o == 0),
                     stop=(o == PASSES - 1),
                 )
 
-        every = range(QUARTERS)
-        part_words(0, 0, "words00")
-        quantise(0, 0, nc.scalar.copy)
-        part_words(0, 1, "rounded0")
+        every, last = range(QUARTERS), QUARTERS - 1
+        quantise(0, 0, nc.scalar.copy, "rounded_first")
         score(0, 0, every)
-        quantise(0, 1, nc.scalar.copy)
-        bias.append(stage.tile([P, HALF], F32, name="bias1", offset=0, align_bytes=64))
-        nc.scalar.copy(out=bias[1][:], in_=spread[1][:])
-        score(0, 1, every)
-        part_words(1, 0, "rounded1")
-        quantise(1, 0, nc.vector.tensor_copy)
-        part_words(1, 1, "rounded2")
+        quantise(0, 1, nc.scalar.copy, "rounded_second")
+        score(0, 1, every[:last])
+        quantise(1, 0, nc.vector.tensor_copy, "rounded_first")
         score(1, 0, every)
-        quantise(1, 1, nc.scalar.copy)
+        quantise(1, 1, nc.scalar.copy, "rounded_last")
+        copy_bias(1, "raw1")
+        score(1, 1, every[:last])
 
-        score(1, 1, every)
-
-        for piece, (c, lo, hi) in enumerate(PIECES):
-            cols = slice(lo, hi)
+        for c, lo, hi in PIECES:
             logit = keep.tile([P, hi - lo], F32, name=f"logit{c}{lo}", align_bytes=64)
             rate = keep.tile([P, hi - lo], F32, name=f"rate{c}{lo}", align_bytes=64)
             result = keep.tile([P, hi - lo], F32, name=f"result{c}{lo}", align_bytes=64)
-            for a in range(lo, hi, P):
+            for j in range(lo // P, hi // P):
+                h, inside = divmod(j, per_half)
+                cols = slice(j * P - lo, (j + 1) * P - lo)
                 nc.vector.tensor_tensor(
-                    out=logit[:, a - lo : a - lo + P], in0=scores[c, a // P][:], in1=bias[a // HALF][:, a % HALF : a % HALF + P], op=ADD
+                    out=logit[:, cols], in0=scores[c, j][:], in1=bias[h][:, inside * P : (inside + 1) * P], op=ADD
                 )
-                nc.scalar.activation(out=rate[:, a - lo : a - lo + P], in_=logit[:, a - lo : a - lo + P], func=EXP)
-            if piece < GPSIMD_PIECES:
-                nc.gpsimd.tensor_scalar(
-                    out=result[:], in0=rate[:], scalar1=exposure[:, c : c + 1], scalar2=0.0, op0=MULT, op1=ADD
-                )
-            else:
-                nc.vector.tensor_scalar_mul(out=result[:], in0=rate[:], scalar1=exposure[:, c : c + 1])
-            nc.sync.dma_start(out=out[0, blocks[c], cols], in_=result[:])
+                if (c, j) == (0, 0):
+                    for o in range(PASSES):
+                        score(o, 1, every[last:])
+                nc.scalar.activation(out=rate[:, cols], in_=logit[:, cols], func=EXP)
+            nc.vector.tensor_scalar_mul(out=result[:], in0=rate[:], scalar1=exposure[:, c : c + 1])
+            nc.sync.dma_start(out=out[0, blocks[c], lo:hi], in_=result[:])

@@ -53,12 +53,9 @@ def tile_attend_rate_topk_kernel(tc, qT, k_words, k_scales, kb, ex, offs, out):
             keep.tile([P, PACK, NQ], F32, name=f"q_raw{o}", tag=f"raw{o}", align_bytes=64) for o in range(PASSES)
         ]
         ident = keep.tile([P, P], F32, name="ident", align_bytes=64)
-        warm_in = keep.tile([P, 1], F32, name="warm_in")
-        warm_out = keep.tile([P, 1], F32, name="warm_out")
         pass1_plane = keep.tile([P, N // 4], I32, name="pass1_plane", align_bytes=64)
 
         nc.gpsimd.memset(scale_pool[:], 0)
-        nc.gpsimd.memset(warm_in[:], 0.0)
         make_identity(nc, ident[:])
         nc.gpsimd.memset(pass1_plane[:], 0)
         nc.vector.memset(kb_pool[0:KB_ROW, :], 0.0)
@@ -71,7 +68,6 @@ def tile_attend_rate_topk_kernel(tc, qT, k_words, k_scales, kb, ex, offs, out):
         for r in range(GROUP):
             nc.sync.dma_start(out=scale_pool[r:P:QUADRANT, :], in_=scale_rows[0, r : GROUP * GROUP : GROUP, :])
         nc.sync.dma_start(out=scale_pool[SPARE_ROW : SPARE_ROW + GROUP * GROUP, :], in_=scale_rows[1])
-        nc.scalar.activation(out=warm_out[:], in_=warm_in[:], func=EXP)
         nc.sync.dma_start(out=word_pool[:, WORDS_FIRST:T], in_=words[:, WORDS_FIRST:T])
         for o in range(PASSES):
             rows = qT[0, o * K_PASS : (o + 1) * K_PASS, :]

@@ -47,31 +47,42 @@ def tile_attend_rate_topk_kernel(tc, qT, k_words, k_scales, kb, ex, offs, out):
 
         offsets = keep.tile([P, N // LIST_GROUP], U16, name="offsets")
         scale_pool = keep.tile([P, T // 4], I32, name="scale_pool", tag="scale_pool", align_bytes=64)
-        kb_pool = keep.tile([P, T], F32, name="kb_pool", align_bytes=64)
+        kb_pool = keep.tile([P, T], F32, name="kb_pool", tag="kb_pool", align_bytes=64)
         word_pool = keep.tile([P, T], I32, name="word_pool", align_bytes=64)
-        q_raw = [
-            keep.tile([P, PACK, NQ], F32, name=f"q_raw{o}", tag=f"raw{o}", align_bytes=64) for o in range(PASSES)
-        ]
         ident = keep.tile([P, P], F32, name="ident", align_bytes=64)
-        pass1_plane = keep.tile([P, N // 4], I32, name="pass1_plane", align_bytes=64)
+        planes = keep.tile([P, PASSES, N // 4], I32, name="planes", align_bytes=64)
 
-        nc.gpsimd.memset(scale_pool[:], 0)
+        nc.gpsimd.memset(scale_pool[32:64, :], 0)
+        nc.gpsimd.memset(scale_pool[64:P, :], 0)
         make_identity(nc, ident[:])
-        nc.gpsimd.memset(pass1_plane[:], 0)
+        nc.gpsimd.memset(planes[:], 0)
         nc.vector.memset(kb_pool[0:KB_ROW, :], 0.0)
 
         nc.sync.dma_start(offsets[:], offs)
+        nc.sync.dma_start(
+            out=scale_pool[0:32, :],
+            in_=k_scales.bitcast(I32).rearrange("o f t -> f o t"),
+        )
         nc.sync.dma_start(out=kb_pool[KB_ROW:P, :], in_=kb[0:1, :])
-        words = k_words[0].rearrange("p t b -> p (t b)").bitcast(I32)
-        nc.sync.dma_start(out=word_pool[:, 0:WORDS_FIRST], in_=words[:, 0:WORDS_FIRST])
-        scale_rows = k_scales.bitcast(I32)
-        for r in range(GROUP):
-            nc.sync.dma_start(out=scale_pool[r:P:QUADRANT, :], in_=scale_rows[0, r : GROUP * GROUP : GROUP, :])
-        nc.sync.dma_start(out=scale_pool[SPARE_ROW : SPARE_ROW + GROUP * GROUP, :], in_=scale_rows[1])
-        nc.sync.dma_start(out=word_pool[:, WORDS_FIRST:T], in_=words[:, WORDS_FIRST:T])
-        for o in range(PASSES):
+        nc.sync.dma_start(out=word_pool[:], in_=k_words[0].rearrange("p t b -> p (t b)").bitcast(I32))
+        q_raw = {}
+
+        def load_queries(o, tag):
+            q_raw[o] = keep.tile([P, PACK, NQ], F32, name=f"q_raw{o}", tag=tag, align_bytes=64)
             rows = qT[0, o * K_PASS : (o + 1) * K_PASS, :]
             nc.sync.dma_start(out=q_raw[o][:], in_=rows.rearrange("(p j) q -> p j q", j=PACK))
+
+        load_queries(0, "raw0")
+
+        listed_scales = keep.tile([P, N], U8, name="listed_scales", align_bytes=64)
+        nc.vector.tensor_copy(out=listed_scales[:], in_=scale_pool[:].bitcast(U8).indirect(offsets[:]))
+        for g in range(GROUP):
+            nc.sync.dma_start(
+                out=planes[QUADRANT * g : QUADRANT * g + GROUP, :, :],
+                in_=listed_scales[8 * g : 8 * g + 8, :].bitcast(I32),
+            )
+        key_scales = [planes[:, o, :].bitcast(U8) for o in range(PASSES)]
+        load_queries(1, "scale_pool")
 
         entries = [offsets[:, h * HALF // LIST_GROUP : (h + 1) * HALF // LIST_GROUP] for h in range(HALVES)]
         slots = [slice(h * HALF, (h + 1) * HALF) for h in range(HALVES)]
@@ -79,9 +90,6 @@ def tile_attend_rate_topk_kernel(tc, qT, k_words, k_scales, kb, ex, offs, out):
         kb_row = [keep.tile([P, HALF], F32, name=f"kb_row{h}", align_bytes=64) for h in range(HALVES)]
         for h in range(HALVES):
             nc.vector.tensor_copy(out=kb_row[h][:], in_=kb_pool[:].indirect(entries[h]))
-
-        listed_scales = keep.tile([P, N], U8, name="listed_scales", align_bytes=64)
-        nc.vector.tensor_copy(out=listed_scales[:], in_=scale_pool[:].bitcast(U8).indirect(offsets[:]))
 
         per_half = QUARTERS // HALVES
         kb_cols = []
@@ -92,15 +100,7 @@ def tile_attend_rate_topk_kernel(tc, qT, k_words, k_scales, kb, ex, offs, out):
             kb_cols.append(keep.tile([P, per_half], F32, name=f"kb_cols{h}", align_bytes=64))
             nc.scalar.copy(out=kb_cols[h][:], in_=turned[:, :, KB_ROW])
 
-        for g in range(GROUP):
-            first = SPARE_ROW + GROUP * g
-            nc.sync.dma_start(
-                out=pass1_plane[QUADRANT * g : QUADRANT * g + GROUP, :],
-                in_=listed_scales[first : first + GROUP, :].bitcast(I32),
-            )
-        key_scales = [listed_scales[:], pass1_plane[:].bitcast(U8)]
-
-        exposure = keep.tile([P, Q_BLOCKS], F32, name="exposure", tag="scale_pool", align_bytes=64)
+        exposure = keep.tile([P, Q_BLOCKS], F32, name="exposure", tag="kb_pool", align_bytes=64)
         with nc.allow_non_contiguous_dma(reason="one exposure a query row"):
             nc.sync.dma_start(out=exposure[:], in_=ex[0].rearrange("(c p) one -> p (c one)", p=P))
 
@@ -174,7 +174,7 @@ def tile_attend_rate_topk_kernel(tc, qT, k_words, k_scales, kb, ex, offs, out):
         quantise(1, 0, nc.vector.tensor_copy, "rounded_first")
         score(1, 0, every)
         quantise(1, 1, nc.scalar.copy, "rounded_last")
-        copy_bias(1, "raw1")
+        copy_bias(1, "scale_pool")
         score(1, 1, every[:last])
 
         for c, lo, hi in PIECES:

@@ -73,6 +73,7 @@ def tile_attend_rate_topk_kernel(tc, qT, k_words, k_scales, kb, ex, offs, out):
             nc.sync.dma_start(out=q_raw[o][:], in_=rows.rearrange("(p j) q -> p j q", j=PACK))
 
         load_queries(0, "raw0")
+        load_queries(1, "raw1")
 
         listed_scales = keep.tile([P, N], U8, name="listed_scales", align_bytes=64)
         nc.vector.tensor_copy(out=listed_scales[:], in_=scale_pool[:].bitcast(U8).indirect(offsets[:]))
@@ -82,7 +83,7 @@ def tile_attend_rate_topk_kernel(tc, qT, k_words, k_scales, kb, ex, offs, out):
                 in_=listed_scales[8 * g : 8 * g + 8, :].bitcast(I32),
             )
         key_scales = [planes[:, o, :].bitcast(U8) for o in range(PASSES)]
-        load_queries(1, "scale_pool")
+
 
         entries = [offsets[:, h * HALF // LIST_GROUP : (h + 1) * HALF // LIST_GROUP] for h in range(HALVES)]
         slots = [slice(h * HALF, (h + 1) * HALF) for h in range(HALVES)]
@@ -174,7 +175,7 @@ def tile_attend_rate_topk_kernel(tc, qT, k_words, k_scales, kb, ex, offs, out):
         quantise(1, 0, nc.vector.tensor_copy, "rounded_first")
         score(1, 0, every)
         quantise(1, 1, nc.scalar.copy, "rounded_last")
-        copy_bias(1, "scale_pool")
+        copy_bias(1, "raw1")
         score(1, 1, every[:last])
 
         for c, lo, hi in PIECES:

@@ -1,7 +1,6 @@
 from contextlib import ExitStack
 
 import concourse.mybir as mybir
-from concourse.masks import make_identity
 
 T, D, NQ, N = 2048, 1024, 256, 512
 FLOPS = 2 * NQ * N * D
@@ -16,6 +15,9 @@ U8 = mybir.dt.uint8
 FP8X4 = mybir.dt.float8_e4m3fn_x4
 FP4X4 = mybir.dt.float4_e2m1fn_x4
 EXP = mybir.ActivationFunctionType.Exp
+COPY = mybir.ActivationFunctionType.Copy
+ABS = mybir.ActivationFunctionType.Abs
+RELU = mybir.ActivationFunctionType.Relu
 ADD = mybir.AluOpType.add
 
 P = 128
@@ -33,7 +35,7 @@ SPARE_ROW = GROUP
 KB_ROW = P - 1
 LINE = 4
 WORDS_FIRST = 896
-SCORE_BANKS = ((0, 1, 2, 3), (4, 5, 6, 0))
+SCORE_BANKS = ((0, 1, 2, 3), (4, 5, 6, 7))
 TURN_BANKS = (4, 5)
 SPREAD_BANKS = (6, 7)
 PIECES = ((0, 0, 256), (0, 256, 512), (1, 0, 256), (1, 256, 384), (1, 384, 512))
@@ -43,21 +45,31 @@ def tile_attend_rate_topk_kernel(tc, qT, k_words, k_scales, kb, ex, offs, out):
     nc = tc.nc
     with ExitStack() as ctx:
         keep = ctx.enter_context(tc.tile_pool(name="keep", bufs=1))
+        held = ctx.enter_context(tc.tile_pool(name="held", bufs=1))
         psum = ctx.enter_context(tc.psum_pool(name="psum", bufs=1))
 
         offsets = keep.tile([P, N // LIST_GROUP], U16, name="offsets")
         scale_pool = keep.tile([P, T // 4], I32, name="scale_pool", tag="scale_pool", align_bytes=64)
         kb_pool = keep.tile([P, T], F32, name="kb_pool", tag="kb_pool", align_bytes=64)
-        word_pool = keep.tile([P, T], I32, name="word_pool", align_bytes=64)
+        word_pool = keep.tile([P, T], I32, name="word_pool", tag="word_pool", align_bytes=64)
         ident = keep.tile([P, P], F32, name="ident", align_bytes=64)
-        planes = keep.tile([P, PASSES, N // 4], I32, name="planes", align_bytes=64)
+
 
         nc.gpsimd.memset(scale_pool[32:64, :], 0)
         nc.gpsimd.memset(scale_pool[64:P, :], 0)
-        make_identity(nc, ident[:])
+        distance = held.tile([P, P], F32, name="distance", offset=10240, align_bytes=64)
+        apart = held.tile([P, P], F32, name="apart", offset=3648, align_bytes=64)
+        nc.gpsimd.iota(distance[:], [[1, P]], base=0, channel_multiplier=-1, allow_small_or_imprecise_dtypes=True)
+        nc.scalar.activation(out=apart[:], in_=distance[:], func=ABS)
+        nc.scalar.activation(out=ident[:], in_=apart[:], func=RELU, scale=-1.0, bias=1.0)
+        planes = keep.tile([P, PASSES, N // 4], I32, name="planes", align_bytes=64)
         nc.gpsimd.memset(planes[:], 0)
         nc.vector.memset(kb_pool[0:KB_ROW, :], 0.0)
 
+        q_raw = [
+            keep.tile([P, PACK, NQ], F32, name="q_raw0", align_bytes=64),
+            held.tile([P, PACK, NQ], F32, name="q_raw1", offset=10752, align_bytes=64),
+        ]
         nc.sync.dma_start(offsets[:], offs)
         nc.sync.dma_start(
             out=scale_pool[0:32, :],
@@ -65,15 +77,13 @@ def tile_attend_rate_topk_kernel(tc, qT, k_words, k_scales, kb, ex, offs, out):
         )
         nc.sync.dma_start(out=kb_pool[KB_ROW:P, :], in_=kb[0:1, :])
         nc.sync.dma_start(out=word_pool[:], in_=k_words[0].rearrange("p t b -> p (t b)").bitcast(I32))
-        q_raw = {}
 
-        def load_queries(o, tag):
-            q_raw[o] = keep.tile([P, PACK, NQ], F32, name=f"q_raw{o}", tag=tag, align_bytes=64)
+        def load_queries(o, places):
             rows = qT[0, o * K_PASS : (o + 1) * K_PASS, :]
-            nc.sync.dma_start(out=q_raw[o][:], in_=rows.rearrange("(p j) q -> p j q", j=PACK))
+            nc.sync.dma_start(out=q_raw[o][:, places, :], in_=rows.rearrange("(p j) q -> p j q", j=PACK)[:, places, :])
 
-        load_queries(0, "raw0")
-        load_queries(1, "raw1")
+        load_queries(0, slice(0, PACK))
+        load_queries(1, slice(0, PACK))
 
         listed_scales = keep.tile([P, N], U8, name="listed_scales", align_bytes=64)
         nc.vector.tensor_copy(out=listed_scales[:], in_=scale_pool[:].bitcast(U8).indirect(offsets[:]))
@@ -88,9 +98,11 @@ def tile_attend_rate_topk_kernel(tc, qT, k_words, k_scales, kb, ex, offs, out):
         entries = [offsets[:, h * HALF // LIST_GROUP : (h + 1) * HALF // LIST_GROUP] for h in range(HALVES)]
         slots = [slice(h * HALF, (h + 1) * HALF) for h in range(HALVES)]
 
-        kb_row = [keep.tile([P, HALF], F32, name=f"kb_row{h}", align_bytes=64) for h in range(HALVES)]
+        second_row = held.tile([P, HALF], F32, name="second_row", offset=3136, align_bytes=64)
+        first_row = held.tile([P, HALF], F32, name="first_row", offset=9344, align_bytes=64)
+        kb_row = [first_row[:], second_row[:]]
         for h in range(HALVES):
-            nc.vector.tensor_copy(out=kb_row[h][:], in_=kb_pool[:].indirect(entries[h]))
+            nc.scalar.activation(out=kb_row[h], in_=kb_pool[:].indirect(entries[h]), func=COPY)
 
         per_half = QUARTERS // HALVES
         kb_cols = []
@@ -98,12 +110,8 @@ def tile_attend_rate_topk_kernel(tc, qT, k_words, k_scales, kb, ex, offs, out):
             turned = psum.tile([P, per_half, P], F32, name=f"turned{h}", tag=f"bank{TURN_BANKS[h]}")
             for j in range(per_half):
                 nc.tensor.transpose(turned[:, j, :], kb_row[h][:, j * P : (j + 1) * P], ident[:])
-            kb_cols.append(keep.tile([P, per_half], F32, name=f"kb_cols{h}", align_bytes=64))
-            nc.scalar.copy(out=kb_cols[h][:], in_=turned[:, :, KB_ROW])
-
-        exposure = keep.tile([P, Q_BLOCKS], F32, name="exposure", tag="kb_pool", align_bytes=64)
-        with nc.allow_non_contiguous_dma(reason="one exposure a query row"):
-            nc.sync.dma_start(out=exposure[:], in_=ex[0].rearrange("(c p) one -> p (c one)", p=P))
+            kb_cols.append(held.tile([P, 32], F32, name=f"kb_cols{h}", offset=(5056, 8192)[h], align_bytes=64))
+            nc.scalar.copy(out=kb_cols[h][:, 0:per_half], in_=turned[:, :, KB_ROW])
 
         spread = []
         for h in range(HALVES):
@@ -113,6 +121,10 @@ def tile_attend_rate_topk_kernel(tc, qT, k_words, k_scales, kb, ex, offs, out):
                     spread[h][:, j * P : (j + 1) * P], kb_cols[h][:, j : j + 1].to_broadcast([P, P]), ident[:]
                 )
 
+        exposure = held.tile([P, Q_BLOCKS], F32, name="exposure", offset=8192, align_bytes=64)
+        with nc.allow_non_contiguous_dma(reason="one exposure a query row"):
+            nc.sync.dma_start(out=exposure[:], in_=ex[0].rearrange("(c p) one -> p (c one)", p=P))
+
         bias = {}
 
         def copy_bias(h, tag):
@@ -120,6 +132,7 @@ def tile_attend_rate_topk_kernel(tc, qT, k_words, k_scales, kb, ex, offs, out):
             nc.scalar.copy(out=bias[h][:], in_=spread[h][:])
 
         copy_bias(0, "bias0")
+        copy_bias(1, "bias1")
 
         word_pairs = keep.tile([P, N], U32, name="word_pairs", align_bytes=64)
         for h in range(HALVES):
@@ -127,23 +140,30 @@ def tile_attend_rate_topk_kernel(tc, qT, k_words, k_scales, kb, ex, offs, out):
 
         by_pass = word_pairs[:].bitcast(U16).rearrange("p (i o) -> p o i", o=PASSES)
         key_words = {}
-        for o in range(PASSES):
-            for h in range(HALVES):
-                key_words[o, h] = keep.tile([P, 2 * HALF], U8, name=f"key_words{o}{h}", align_bytes=64)
-                nc.vector.tensor_copy(out=key_words[o, h][:].bitcast(U16), in_=by_pass[:, o, slots[h]])
+
+        def part(o, h, pool, **place):
+            key_words[o, h] = pool.tile([P, 2 * HALF], U8, name=f"key_words{o}{h}", align_bytes=64, **place)
+            nc.vector.tensor_copy(out=key_words[o, h][:].bitcast(U16), in_=by_pass[:, o, slots[h]])
+
+        for h in range(HALVES):
+            part(0, h, keep)
 
         blocks = [slice(c * P, (c + 1) * P) for c in range(Q_BLOCKS)]
         scores = {}
         quantised = {}
 
-        def quantise(o, c, copy, tag):
-            q_bf = keep.tile([P, P, PACK], BF16, name=f"q_bf{o}{c}", tag=tag, align_bytes=64)
-            q_codes = keep.tile([P, P], U32, name=f"q_codes{o}{c}", align_bytes=64)
+        def rounded(o, c, shares, pool, **place):
+            q_bf = pool.tile([P, P, PACK], BF16, name=f"q_bf{o}{c}", align_bytes=64, **place)
+            for copy, lo, hi in shares:
+                copy(
+                    out=q_bf[:, lo:hi, :].rearrange("p (a i) j -> p a j i", i=LINE),
+                    in_=q_raw[o][:, :, c * P + lo : c * P + hi].rearrange("p j (a i) -> p a j i", i=LINE),
+                )
+            return q_bf
+
+        def quantise(o, c, q_bf, pool, **place):
+            q_codes = pool.tile([P, P], U32, name=f"q_codes{o}{c}", align_bytes=64, **place)
             q_scales = keep.tile([P, P], U8, name=f"q_scales{o}{c}", align_bytes=64)
-            copy(
-                out=q_bf[:].rearrange("p (a i) j -> p a j i", i=LINE),
-                in_=q_raw[o][:, :, blocks[c]].rearrange("p j (a i) -> p a j i", i=LINE),
-            )
             nc.vector.quantize_mx(
                 out=q_codes[:].bitcast(FP8X4),
                 scales=q_scales[:],
@@ -151,9 +171,9 @@ def tile_attend_rate_topk_kernel(tc, qT, k_words, k_scales, kb, ex, offs, out):
             )
             quantised[o, c] = (q_codes, q_scales)
 
-        def score(o, c, quarters):
+        def score(o, c):
             q_codes, q_scales = quantised[o, c]
-            for j in quarters:
+            for j in range(QUARTERS):
                 if o == 0:
                     scores[c, j] = psum.tile([P, P], F32, name=f"scores{c}{j}", tag=f"bank{SCORE_BANKS[c][j]}")
                 h, inside = divmod(j, per_half)
@@ -167,16 +187,21 @@ def tile_attend_rate_topk_kernel(tc, qT, k_words, k_scales, kb, ex, offs, out):
                     stop=(o == PASSES - 1),
                 )
 
-        every, last = range(QUARTERS), QUARTERS - 1
-        quantise(0, 0, nc.scalar.copy, "rounded_first")
-        score(0, 0, every)
-        quantise(0, 1, nc.scalar.copy, "rounded_second")
-        score(0, 1, every[:last])
-        quantise(1, 0, nc.vector.tensor_copy, "rounded_first")
-        score(1, 0, every)
-        quantise(1, 1, nc.scalar.copy, "rounded_last")
-        copy_bias(1, "raw1")
-        score(1, 1, every[:last])
+        on_scalar, on_vector = nc.scalar.copy, nc.vector.tensor_copy
+        first = rounded(0, 0, [(on_scalar, 0, P)], held, offset=4096)
+        second = rounded(0, 1, [(on_vector, 0, P)], keep, tag="word_pool")
+        quantise(0, 0, first, keep)
+        score(0, 0)
+        quantise(0, 1, second, held, offset=4160)
+        score(0, 1)
+        part(1, 0, held, offset=3648)
+        third = rounded(1, 0, [(on_scalar, 0, P // 2), (on_vector, P // 2, P)], held, offset=4672)
+        fourth = rounded(1, 1, [(on_vector, 0, P)], keep, tag="word_pool")
+        quantise(1, 0, third, keep)
+        part(1, 1, held, offset=10752)
+        score(1, 0)
+        quantise(1, 1, fourth, held, offset=11264)
+        score(1, 1)
 
         for c, lo, hi in PIECES:
             logit = keep.tile([P, hi - lo], F32, name=f"logit{c}{lo}", align_bytes=64)
@@ -188,9 +213,6 @@ def tile_attend_rate_topk_kernel(tc, qT, k_words, k_scales, kb, ex, offs, out):
                 nc.vector.tensor_tensor(
                     out=logit[:, cols], in0=scores[c, j][:], in1=bias[h][:, inside * P : (inside + 1) * P], op=ADD
                 )
-                if (c, j) == (0, 0):
-                    for o in range(PASSES):
-                        score(o, 1, every[last:])
                 nc.scalar.activation(out=rate[:, cols], in_=logit[:, cols], func=EXP)
             nc.vector.tensor_scalar_mul(out=result[:], in0=rate[:], scalar1=exposure[:, c : c + 1])
             nc.sync.dma_start(out=out[0, blocks[c], lo:hi], in_=result[:])

@@ -37,7 +37,6 @@ LINE = 4
 WORDS_FIRST = 896
 SCORE_BANKS = ((0, 1, 2, 3), (4, 5, 6, 7))
 TURN_BANKS = (4, 5)
-SPREAD_BANKS = (6, 7)
 PIECES = ((0, 0, 256), (0, 256, 512), (1, 0, 256), (1, 256, 384), (1, 384, 512))
 
 
@@ -57,17 +56,18 @@ def tile_attend_rate_topk_kernel(tc, qT, k_words, k_scales, kb, ex, offs, out):
 
         nc.gpsimd.memset(scale_pool[32:64, :], 0)
         nc.gpsimd.memset(scale_pool[64:P, :], 0)
-        distance = held.tile([P, P], F32, name="distance", offset=10240, align_bytes=64)
-        apart = held.tile([P, P], F32, name="apart", offset=3648, align_bytes=64)
+        distance = held.tile([P, P], F32, name="distance", offset=3648, align_bytes=64)
+        apart = held.tile([P, P], F32, name="apart", offset=10240, align_bytes=64)
         nc.gpsimd.iota(distance[:], [[1, P]], base=0, channel_multiplier=-1, allow_small_or_imprecise_dtypes=True)
         nc.scalar.activation(out=apart[:], in_=distance[:], func=ABS)
         nc.scalar.activation(out=ident[:], in_=apart[:], func=RELU, scale=-1.0, bias=1.0)
         planes = keep.tile([P, PASSES, N // 4], I32, name="planes", align_bytes=64)
         nc.gpsimd.memset(planes[:], 0)
-        nc.vector.memset(kb_pool[0:KB_ROW, :], 0.0)
+        nc.vector.memset(kb_pool[0:KB_ROW, 0 : T // 2 + 1], 0.0)
+        nc.vector.memset(kb_pool[0:KB_ROW, T // 2 + 1 : T], 0.0)
 
         q_raw = [
-            keep.tile([P, PACK, NQ], F32, name="q_raw0", align_bytes=64),
+            keep.tile([P, PACK, NQ], F32, name="q_raw0", tag="raw0", align_bytes=64),
             held.tile([P, PACK, NQ], F32, name="q_raw1", offset=10752, align_bytes=64),
         ]
         nc.sync.dma_start(offsets[:], offs)
@@ -98,41 +98,41 @@ def tile_attend_rate_topk_kernel(tc, qT, k_words, k_scales, kb, ex, offs, out):
         entries = [offsets[:, h * HALF // LIST_GROUP : (h + 1) * HALF // LIST_GROUP] for h in range(HALVES)]
         slots = [slice(h * HALF, (h + 1) * HALF) for h in range(HALVES)]
 
-        second_row = held.tile([P, HALF], F32, name="second_row", offset=3136, align_bytes=64)
-        first_row = held.tile([P, HALF], F32, name="first_row", offset=9344, align_bytes=64)
+        second_row = held.tile([P, HALF], F32, name="second_row", offset=9344, align_bytes=64)
+        first_row = held.tile([P, HALF], F32, name="first_row", offset=3136, align_bytes=64)
         kb_row = [first_row[:], second_row[:]]
         for h in range(HALVES):
             nc.scalar.activation(out=kb_row[h], in_=kb_pool[:].indirect(entries[h]), func=COPY)
 
         per_half = QUARTERS // HALVES
-        kb_cols = []
+        turned = []
         for h in range(HALVES):
-            turned = psum.tile([P, per_half, P], F32, name=f"turned{h}", tag=f"bank{TURN_BANKS[h]}")
+            turned.append(psum.tile([P, per_half, P], F32, name=f"turned{h}", tag=f"bank{TURN_BANKS[h]}"))
             for j in range(per_half):
-                nc.tensor.transpose(turned[:, j, :], kb_row[h][:, j * P : (j + 1) * P], ident[:])
-            kb_cols.append(held.tile([P, 32], F32, name=f"kb_cols{h}", offset=(5056, 8192)[h], align_bytes=64))
-            nc.scalar.copy(out=kb_cols[h][:, 0:per_half], in_=turned[:, :, KB_ROW])
+                nc.tensor.transpose(turned[h][:, j, :], kb_row[h][:, j * P : (j + 1) * P], ident[:])
 
-        spread = []
-        for h in range(HALVES):
-            spread.append(psum.tile([P, HALF], F32, name=f"spread{h}", tag=f"bank{SPREAD_BANKS[h]}"))
+        spread = {}
+
+        def spread_biases(h):
+            kb_cols = held.tile([P, 32], F32, name=f"kb_cols{h}", offset=(8192, 8320)[h], align_bytes=64)
+            nc.scalar.copy(out=kb_cols[:, 0:per_half], in_=turned[h][:, :, KB_ROW])
+            if h == 0:
+                both = psum.tile([P, HALF], F32, name="spread0", tag="bank4")
+                spread[0], spread[1] = both[:, 0:P], both[:, P:HALF]
+                spread["first"] = both[:]
+            else:
+                for j in range(per_half):
+                    spread[2 + j] = psum.tile([P, P], F32, name=f"spread{2 + j}", tag=f"bank{6 + j}")[:]
             for j in range(per_half):
-                nc.tensor.transpose(
-                    spread[h][:, j * P : (j + 1) * P], kb_cols[h][:, j : j + 1].to_broadcast([P, P]), ident[:]
-                )
+                nc.tensor.transpose(spread[2 * h + j], kb_cols[:, j : j + 1].to_broadcast([P, P]), ident[:])
+
+        spread_biases(0)
 
         exposure = held.tile([P, Q_BLOCKS], F32, name="exposure", offset=8192, align_bytes=64)
         with nc.allow_non_contiguous_dma(reason="one exposure a query row"):
             nc.sync.dma_start(out=exposure[:], in_=ex[0].rearrange("(c p) one -> p (c one)", p=P))
 
         bias = {}
-
-        def copy_bias(h, tag):
-            bias[h] = keep.tile([P, HALF], F32, name=f"bias{h}", tag=tag, align_bytes=64)
-            nc.scalar.copy(out=bias[h][:], in_=spread[h][:])
-
-        copy_bias(0, "bias0")
-        copy_bias(1, "bias1")
 
         word_pairs = keep.tile([P, N], U32, name="word_pairs", align_bytes=64)
         for h in range(HALVES):
@@ -171,9 +171,9 @@ def tile_attend_rate_topk_kernel(tc, qT, k_words, k_scales, kb, ex, offs, out):
             )
             quantised[o, c] = (q_codes, q_scales)
 
-        def score(o, c):
+        def score(o, c, quarters):
             q_codes, q_scales = quantised[o, c]
-            for j in range(QUARTERS):
+            for j in quarters:
                 if o == 0:
                     scores[c, j] = psum.tile([P, P], F32, name=f"scores{c}{j}", tag=f"bank{SCORE_BANKS[c][j]}")
                 h, inside = divmod(j, per_half)
@@ -188,23 +188,36 @@ def tile_attend_rate_topk_kernel(tc, qT, k_words, k_scales, kb, ex, offs, out):
                 )
 
         on_scalar, on_vector = nc.scalar.copy, nc.vector.tensor_copy
+        every = range(QUARTERS)
         first = rounded(0, 0, [(on_scalar, 0, P)], held, offset=4096)
+        spread_biases(1)
+        bias[0] = keep.tile([P, HALF], F32, name="bias0", align_bytes=64)
+        nc.scalar.copy(out=bias[0][:], in_=spread["first"])
         second = rounded(0, 1, [(on_vector, 0, P)], keep, tag="word_pool")
         quantise(0, 0, first, keep)
-        score(0, 0)
+        score(0, 0, every)
+        third = rounded(1, 0, [(on_vector, 0, P)], held, offset=4672)
         quantise(0, 1, second, held, offset=4160)
-        score(0, 1)
+        score(0, 1, every[:per_half])
         part(1, 0, held, offset=3648)
-        third = rounded(1, 0, [(on_scalar, 0, P // 2), (on_vector, P // 2, P)], held, offset=4672)
-        fourth = rounded(1, 1, [(on_vector, 0, P)], keep, tag="word_pool")
         quantise(1, 0, third, keep)
-        part(1, 1, held, offset=10752)
-        score(1, 0)
-        quantise(1, 1, fourth, held, offset=11264)
-        score(1, 1)
+        part(1, 1, keep, tag="word_pool")
+        fourth = rounded(1, 1, [(on_scalar, 0, P)], keep, tag="raw0")
+        score(1, 0, every)
+        quantise(1, 1, fourth, keep)
+        bias[1] = held.tile([P, HALF], F32, name="bias1", offset=12800, align_bytes=64)
+        for j in range(per_half):
+            nc.scalar.copy(out=bias[1][:, j * P : (j + 1) * P], in_=spread[per_half + j])
+        score(1, 1, every[:per_half])
+        for j in every[per_half:]:
+            for o in range(PASSES):
+                score(o, 1, [j])
 
         for c, lo, hi in PIECES:
-            logit = keep.tile([P, hi - lo], F32, name=f"logit{c}{lo}", align_bytes=64)
+            if c == 0:
+                logit = held.tile([P, hi - lo], F32, name=f"logit{c}{lo}", offset=10752 + 4 * lo, align_bytes=64)
+            else:
+                logit = keep.tile([P, hi - lo], F32, name=f"logit{c}{lo}", align_bytes=64)
             rate = keep.tile([P, hi - lo], F32, name=f"rate{c}{lo}", align_bytes=64)
             result = keep.tile([P, hi - lo], F32, name=f"result{c}{lo}", align_bytes=64)
             for j in range(lo // P, hi // P):

@@ -28,146 +28,130 @@ Q_BLOCKS = NQ // P
 QUARTERS = N // P
 HALVES = 2
 HALF = N // HALVES
+PER_HALF = QUARTERS // HALVES
 LIST_GROUP = 16
 QUADRANT = 32
 GROUP = 4
-SPARE_ROW = GROUP
+SCALE_ROWS = PASSES * GROUP * GROUP
 KB_ROW = P - 1
+ODD_SPLIT = T // 2 + 1
 LINE = 4
-WORDS_FIRST = 896
-SCORE_BANKS = ((0, 1, 2, 3), (4, 5, 6, 7))
-TURN_BANKS = (4, 5)
 PIECES = ((0, 0, 256), (0, 256, 512), (1, 0, 256), (1, 256, 384), (1, 384, 512))
+
+KIB = 1024
+FIRST_CHAIN = 0
+SECOND_CHAIN = 1 * KIB
+COLUMNS = 2 * KIB
+RAW = (4 * KIB, 8 * KIB)
 
 
 def tile_attend_rate_topk_kernel(tc, qT, k_words, k_scales, kb, ex, offs, out):
     nc = tc.nc
     with ExitStack() as ctx:
         keep = ctx.enter_context(tc.tile_pool(name="keep", bufs=1))
-        held = ctx.enter_context(tc.tile_pool(name="held", bufs=1))
+        shared = ctx.enter_context(tc.tile_pool(name="shared", bufs=1))
         psum = ctx.enter_context(tc.psum_pool(name="psum", bufs=1))
 
+        def sbuf(shape, dtype, name, at=None):
+            if at is None:
+                return keep.tile(shape, dtype, name=name, align_bytes=64)
+            return shared.tile(shape, dtype, name=name, offset=at, align_bytes=64)
+
+        def bank(columns, name, number):
+            return psum.tile([P, columns], F32, name=name, tag=f"bank{number}")
+
         offsets = keep.tile([P, N // LIST_GROUP], U16, name="offsets")
-        scale_pool = keep.tile([P, T // 4], I32, name="scale_pool", tag="scale_pool", align_bytes=64)
-        kb_pool = keep.tile([P, T], F32, name="kb_pool", tag="kb_pool", align_bytes=64)
-        word_pool = keep.tile([P, T], I32, name="word_pool", tag="word_pool", align_bytes=64)
-        ident = keep.tile([P, P], F32, name="ident", align_bytes=64)
+        scale_pool = sbuf([P, T // 4], I32, "scale_pool")
+        kb_pool = sbuf([P, T], F32, "kb_pool")
+        word_pool = sbuf([P, T], I32, "word_pool")
+        ident = sbuf([P, P], F32, "ident")
+        planes = sbuf([P, PASSES, N // 4], I32, "planes")
 
-
-        nc.gpsimd.memset(scale_pool[32:64, :], 0)
-        nc.gpsimd.memset(scale_pool[64:P, :], 0)
-        distance = held.tile([P, P], F32, name="distance", offset=3648, align_bytes=64)
-        apart = held.tile([P, P], F32, name="apart", offset=10240, align_bytes=64)
+        nc.gpsimd.memset(scale_pool[SCALE_ROWS : P // 2, :], 0)
+        nc.gpsimd.memset(scale_pool[P // 2 : P, :], 0)
+        distance = sbuf([P, P], F32, "distance", FIRST_CHAIN)
+        apart = sbuf([P, P], F32, "apart", SECOND_CHAIN)
         nc.gpsimd.iota(distance[:], [[1, P]], base=0, channel_multiplier=-1, allow_small_or_imprecise_dtypes=True)
         nc.scalar.activation(out=apart[:], in_=distance[:], func=ABS)
         nc.scalar.activation(out=ident[:], in_=apart[:], func=RELU, scale=-1.0, bias=1.0)
-        planes = keep.tile([P, PASSES, N // 4], I32, name="planes", align_bytes=64)
         nc.gpsimd.memset(planes[:], 0)
-        nc.vector.memset(kb_pool[0:KB_ROW, 0 : T // 2 + 1], 0.0)
-        nc.vector.memset(kb_pool[0:KB_ROW, T // 2 + 1 : T], 0.0)
+        nc.vector.memset(kb_pool[0:KB_ROW, 0:ODD_SPLIT], 0.0)
+        nc.vector.memset(kb_pool[0:KB_ROW, ODD_SPLIT:T], 0.0)
 
-        q_raw = [
-            keep.tile([P, PACK, NQ], F32, name="q_raw0", tag="raw0", align_bytes=64),
-            held.tile([P, PACK, NQ], F32, name="q_raw1", offset=10752, align_bytes=64),
-        ]
         nc.sync.dma_start(offsets[:], offs)
-        nc.sync.dma_start(
-            out=scale_pool[0:32, :],
-            in_=k_scales.bitcast(I32).rearrange("o f t -> f o t"),
-        )
+        nc.sync.dma_start(out=scale_pool[0:SCALE_ROWS, :], in_=k_scales.bitcast(I32).rearrange("o f t -> f o t"))
         nc.sync.dma_start(out=kb_pool[KB_ROW:P, :], in_=kb[0:1, :])
         nc.sync.dma_start(out=word_pool[:], in_=k_words[0].rearrange("p t b -> p (t b)").bitcast(I32))
-
-        def load_queries(o, places):
+        q_raw = []
+        for o in range(PASSES):
+            q_raw.append(sbuf([P, PACK, NQ], F32, f"q_raw{o}", RAW[o]))
             rows = qT[0, o * K_PASS : (o + 1) * K_PASS, :]
-            nc.sync.dma_start(out=q_raw[o][:, places, :], in_=rows.rearrange("(p j) q -> p j q", j=PACK)[:, places, :])
+            nc.sync.dma_start(out=q_raw[o][:], in_=rows.rearrange("(p j) q -> p j q", j=PACK))
 
-        load_queries(0, slice(0, PACK))
-        load_queries(1, slice(0, PACK))
-
-        listed_scales = keep.tile([P, N], U8, name="listed_scales", align_bytes=64)
+        listed_scales = sbuf([P, N], U8, "listed_scales")
         nc.vector.tensor_copy(out=listed_scales[:], in_=scale_pool[:].bitcast(U8).indirect(offsets[:]))
         for g in range(GROUP):
+            source = slice(PASSES * GROUP * g, PASSES * GROUP * (g + 1))
             nc.sync.dma_start(
-                out=planes[QUADRANT * g : QUADRANT * g + GROUP, :, :],
-                in_=listed_scales[8 * g : 8 * g + 8, :].bitcast(I32),
+                out=planes[QUADRANT * g : QUADRANT * g + GROUP, :, :], in_=listed_scales[source, :].bitcast(I32)
             )
         key_scales = [planes[:, o, :].bitcast(U8) for o in range(PASSES)]
 
-
         entries = [offsets[:, h * HALF // LIST_GROUP : (h + 1) * HALF // LIST_GROUP] for h in range(HALVES)]
         slots = [slice(h * HALF, (h + 1) * HALF) for h in range(HALVES)]
+        blocks = [slice(c * P, (c + 1) * P) for c in range(Q_BLOCKS)]
 
-        second_row = held.tile([P, HALF], F32, name="second_row", offset=9344, align_bytes=64)
-        first_row = held.tile([P, HALF], F32, name="first_row", offset=3136, align_bytes=64)
-        kb_row = [first_row[:], second_row[:]]
+        kb_row = [sbuf([P, HALF], F32, f"kb_row{h}", (FIRST_CHAIN, SECOND_CHAIN)[h]) for h in range(HALVES)]
         for h in range(HALVES):
-            nc.scalar.activation(out=kb_row[h], in_=kb_pool[:].indirect(entries[h]), func=COPY)
+            nc.scalar.activation(out=kb_row[h][:], in_=kb_pool[:].indirect(entries[h]), func=COPY)
 
-        per_half = QUARTERS // HALVES
         turned = []
         for h in range(HALVES):
-            turned.append(psum.tile([P, per_half, P], F32, name=f"turned{h}", tag=f"bank{TURN_BANKS[h]}"))
-            for j in range(per_half):
-                nc.tensor.transpose(turned[h][:, j, :], kb_row[h][:, j * P : (j + 1) * P], ident[:])
+            turned.append(bank(HALF, f"turned{h}", QUARTERS + h))
+            for j in range(PER_HALF):
+                nc.tensor.transpose(turned[h][:, j * P : (j + 1) * P], kb_row[h][:, j * P : (j + 1) * P], ident[:])
 
-        spread = {}
+        def bias_columns(h, copy, at=None):
+            columns = sbuf([P, PER_HALF], F32, f"kb_cols{h}", at)
+            copy(out=columns[:], in_=turned[h][:].rearrange("p (j r) -> p j r", r=P)[:, :, KB_ROW])
+            return columns
 
-        def spread_biases(h):
-            kb_cols = held.tile([P, 32], F32, name=f"kb_cols{h}", offset=(8192, 8320)[h], align_bytes=64)
-            nc.scalar.copy(out=kb_cols[:, 0:per_half], in_=turned[h][:, :, KB_ROW])
-            if h == 0:
-                both = psum.tile([P, HALF], F32, name="spread0", tag="bank4")
-                spread[0], spread[1] = both[:, 0:P], both[:, P:HALF]
-                spread["first"] = both[:]
-            else:
-                for j in range(per_half):
-                    spread[2 + j] = psum.tile([P, P], F32, name=f"spread{2 + j}", tag=f"bank{6 + j}")[:]
-            for j in range(per_half):
-                nc.tensor.transpose(spread[2 * h + j], kb_cols[:, j : j + 1].to_broadcast([P, P]), ident[:])
+        def spread(rows, columns, j):
+            nc.tensor.transpose(rows, columns[:, j : j + 1].to_broadcast([P, P]), ident[:])
 
-        spread_biases(0)
+        first_columns = bias_columns(0, nc.scalar.copy, COLUMNS)
+        first_spread = bank(HALF, "first_spread", QUARTERS)
+        for j in range(PER_HALF):
+            spread(first_spread[:, j * P : (j + 1) * P], first_columns, j)
 
-        exposure = held.tile([P, Q_BLOCKS], F32, name="exposure", offset=8192, align_bytes=64)
+        exposure = sbuf([P, Q_BLOCKS], F32, "exposure", COLUMNS)
         with nc.allow_non_contiguous_dma(reason="one exposure a query row"):
             nc.sync.dma_start(out=exposure[:], in_=ex[0].rearrange("(c p) one -> p (c one)", p=P))
 
-        bias = {}
-
-        word_pairs = keep.tile([P, N], U32, name="word_pairs", align_bytes=64)
+        word_pairs = sbuf([P, N], U32, "word_pairs")
         for h in range(HALVES):
             nc.vector.tensor_copy(out=word_pairs[:, slots[h]], in_=word_pool[:].bitcast(U32).indirect(entries[h]))
-
         by_pass = word_pairs[:].bitcast(U16).rearrange("p (i o) -> p o i", o=PASSES)
-        key_words = {}
 
-        def part(o, h, pool, **place):
-            key_words[o, h] = pool.tile([P, 2 * HALF], U8, name=f"key_words{o}{h}", align_bytes=64, **place)
+        key_words, quantised, scores = {}, {}, {}
+
+        def part(o, h, at=None):
+            key_words[o, h] = sbuf([P, 2 * HALF], U8, f"key_words{o}{h}", at)
             nc.vector.tensor_copy(out=key_words[o, h][:].bitcast(U16), in_=by_pass[:, o, slots[h]])
 
-        for h in range(HALVES):
-            part(0, h, keep)
-
-        blocks = [slice(c * P, (c + 1) * P) for c in range(Q_BLOCKS)]
-        scores = {}
-        quantised = {}
-
-        def rounded(o, c, shares, pool, **place):
-            q_bf = pool.tile([P, P, PACK], BF16, name=f"q_bf{o}{c}", align_bytes=64, **place)
-            for copy, lo, hi in shares:
-                copy(
-                    out=q_bf[:, lo:hi, :].rearrange("p (a i) j -> p a j i", i=LINE),
-                    in_=q_raw[o][:, :, c * P + lo : c * P + hi].rearrange("p j (a i) -> p a j i", i=LINE),
-                )
+        def round_queries(o, c, copy, at):
+            q_bf = sbuf([P, P, PACK], BF16, f"q_bf{o}{c}", at)
+            copy(
+                out=q_bf[:].rearrange("p (a i) j -> p a j i", i=LINE),
+                in_=q_raw[o][:, :, blocks[c]].rearrange("p j (a i) -> p a j i", i=LINE),
+            )
             return q_bf
 
-        def quantise(o, c, q_bf, pool, **place):
-            q_codes = pool.tile([P, P], U32, name=f"q_codes{o}{c}", align_bytes=64, **place)
-            q_scales = keep.tile([P, P], U8, name=f"q_scales{o}{c}", align_bytes=64)
+        def quantise(o, c, q_bf, at=None):
+            q_codes = sbuf([P, P], U32, f"q_codes{o}{c}", at)
+            q_scales = sbuf([P, P], U8, f"q_scales{o}{c}")
             nc.vector.quantize_mx(
-                out=q_codes[:].bitcast(FP8X4),
-                scales=q_scales[:],
-                in_=q_bf[:].rearrange("p q j -> p (q j)"),
+                out=q_codes[:].bitcast(FP8X4), scales=q_scales[:], in_=q_bf[:].rearrange("p q j -> p (q j)")
             )
             quantised[o, c] = (q_codes, q_scales)
 
@@ -175,8 +159,8 @@ def tile_attend_rate_topk_kernel(tc, qT, k_words, k_scales, kb, ex, offs, out):
             q_codes, q_scales = quantised[o, c]
             for j in quarters:
                 if o == 0:
-                    scores[c, j] = psum.tile([P, P], F32, name=f"scores{c}{j}", tag=f"bank{SCORE_BANKS[c][j]}")
-                h, inside = divmod(j, per_half)
+                    scores[c, j] = bank(P, f"scores{c}{j}", QUARTERS * c + j)
+                h, inside = divmod(j, PER_HALF)
                 nc.tensor.matmul_mx(
                     out=scores[c, j][:],
                     lhsT=q_codes[:].bitcast(FP8X4),
@@ -187,41 +171,45 @@ def tile_attend_rate_topk_kernel(tc, qT, k_words, k_scales, kb, ex, offs, out):
                     stop=(o == PASSES - 1),
                 )
 
-        on_scalar, on_vector = nc.scalar.copy, nc.vector.tensor_copy
         every = range(QUARTERS)
-        first = rounded(0, 0, [(on_scalar, 0, P)], held, offset=4096)
-        spread_biases(1)
-        bias[0] = keep.tile([P, HALF], F32, name="bias0", align_bytes=64)
-        nc.scalar.copy(out=bias[0][:], in_=spread["first"])
-        second = rounded(0, 1, [(on_vector, 0, P)], keep, tag="word_pool")
-        quantise(0, 0, first, keep)
+        early, late = every[:PER_HALF], every[PER_HALF:]
+        for h in range(HALVES):
+            part(0, h)
+
+        rounded_00 = round_queries(0, 0, nc.scalar.copy, FIRST_CHAIN)
+        second_columns = bias_columns(1, nc.vector.tensor_copy)
+        second_spread = [bank(P, f"second_spread{j}", QUARTERS + j) for j in late]
+        for j in range(PER_HALF):
+            spread(second_spread[j][:], second_columns, j)
+        bias = [sbuf([P, HALF], F32, "bias0")]
+        nc.scalar.copy(out=bias[0][:], in_=first_spread[:])
+        rounded_01 = round_queries(0, 1, nc.vector.tensor_copy, SECOND_CHAIN)
+        quantise(0, 0, rounded_00)
         score(0, 0, every)
-        third = rounded(1, 0, [(on_vector, 0, P)], held, offset=4672)
-        quantise(0, 1, second, held, offset=4160)
-        score(0, 1, every[:per_half])
-        part(1, 0, held, offset=3648)
-        quantise(1, 0, third, keep)
-        part(1, 1, keep, tag="word_pool")
-        fourth = rounded(1, 1, [(on_scalar, 0, P)], keep, tag="raw0")
+
+        rounded_10 = round_queries(1, 0, nc.vector.tensor_copy, RAW[0])
+        quantise(0, 1, rounded_01, RAW[0] + KIB)
+        score(0, 1, early)
+        part(1, 0, RAW[0] + KIB + KIB // 2)
+        quantise(1, 0, rounded_10)
+        part(1, 1, SECOND_CHAIN)
+        rounded_11 = round_queries(1, 1, nc.scalar.copy, RAW[0] + 2 * KIB)
         score(1, 0, every)
-        quantise(1, 1, fourth, keep)
-        bias[1] = held.tile([P, HALF], F32, name="bias1", offset=12800, align_bytes=64)
-        for j in range(per_half):
-            nc.scalar.copy(out=bias[1][:, j * P : (j + 1) * P], in_=spread[per_half + j])
-        score(1, 1, every[:per_half])
-        for j in every[per_half:]:
+        quantise(1, 1, rounded_11)
+        bias.append(sbuf([P, HALF], F32, "bias1", RAW[1] + 2 * KIB))
+        for j in range(PER_HALF):
+            nc.scalar.copy(out=bias[1][:, j * P : (j + 1) * P], in_=second_spread[j][:])
+        score(1, 1, early)
+        for j in late:
             for o in range(PASSES):
                 score(o, 1, [j])
 
         for c, lo, hi in PIECES:
-            if c == 0:
-                logit = held.tile([P, hi - lo], F32, name=f"logit{c}{lo}", offset=10752 + 4 * lo, align_bytes=64)
-            else:
-                logit = keep.tile([P, hi - lo], F32, name=f"logit{c}{lo}", align_bytes=64)
-            rate = keep.tile([P, hi - lo], F32, name=f"rate{c}{lo}", align_bytes=64)
-            result = keep.tile([P, hi - lo], F32, name=f"result{c}{lo}", align_bytes=64)
+            logit = sbuf([P, hi - lo], F32, f"logit{c}{lo}", RAW[1] + 4 * lo if c == 0 else None)
+            rate = sbuf([P, hi - lo], F32, f"rate{c}{lo}")
+            result = sbuf([P, hi - lo], F32, f"result{c}{lo}")
             for j in range(lo // P, hi // P):
-                h, inside = divmod(j, per_half)
+                h, inside = divmod(j, PER_HALF)
                 cols = slice(j * P - lo, (j + 1) * P - lo)
                 nc.vector.tensor_tensor(
                     out=logit[:, cols], in0=scores[c, j][:], in1=bias[h][:, inside * P : (inside + 1) * P], op=ADD

@@ -19,6 +19,7 @@ COPY = mybir.ActivationFunctionType.Copy
 ABS = mybir.ActivationFunctionType.Abs
 RELU = mybir.ActivationFunctionType.Relu
 ADD = mybir.AluOpType.add
+MULT = mybir.AluOpType.mult
 
 P = 128
 PACK = 4
@@ -172,7 +173,7 @@ def tile_attend_rate_topk_kernel(tc, qT, k_words, k_scales, kb, ex, offs, out):
                 )
 
         every = range(QUARTERS)
-        early, late = every[:PER_HALF], every[PER_HALF:]
+        late = every[PER_HALF:]
         for h in range(HALVES):
             part(0, h)
 
@@ -188,19 +189,17 @@ def tile_attend_rate_topk_kernel(tc, qT, k_words, k_scales, kb, ex, offs, out):
         score(0, 0, every)
 
         rounded_10 = round_queries(1, 0, nc.vector.tensor_copy, RAW[0])
-        quantise(0, 1, rounded_01, RAW[0] + KIB)
-        score(0, 1, early)
         part(1, 0, RAW[0] + KIB + KIB // 2)
         quantise(1, 0, rounded_10)
-        part(1, 1, SECOND_CHAIN)
-        rounded_11 = round_queries(1, 1, nc.scalar.copy, RAW[0] + 2 * KIB)
+        part(1, 1, RAW[0] + KIB)
         score(1, 0, every)
+        quantise(0, 1, rounded_01, RAW[0])
+        rounded_11 = round_queries(1, 1, nc.scalar.copy, RAW[0] + 2 * KIB)
         quantise(1, 1, rounded_11)
         bias.append(sbuf([P, HALF], F32, "bias1", RAW[1] + 2 * KIB))
         for j in range(PER_HALF):
             nc.scalar.copy(out=bias[1][:, j * P : (j + 1) * P], in_=second_spread[j][:])
-        score(1, 1, early)
-        for j in late:
+        for j in every:
             for o in range(PASSES):
                 score(o, 1, [j])
 
@@ -215,5 +214,10 @@ def tile_attend_rate_topk_kernel(tc, qT, k_words, k_scales, kb, ex, offs, out):
                     out=logit[:, cols], in0=scores[c, j][:], in1=bias[h][:, inside * P : (inside + 1) * P], op=ADD
                 )
                 nc.scalar.activation(out=rate[:, cols], in_=logit[:, cols], func=EXP)
-            nc.vector.tensor_scalar_mul(out=result[:], in0=rate[:], scalar1=exposure[:, c : c + 1])
+            if (c, lo) == (0, 0):
+                nc.gpsimd.tensor_scalar(
+                    out=result[:], in0=rate[:], scalar1=exposure[:, 0:1], scalar2=0.0, op0=MULT, op1=ADD
+                )
+            else:
+                nc.vector.tensor_scalar_mul(out=result[:], in0=rate[:], scalar1=exposure[:, c : c + 1])
             nc.sync.dma_start(out=out[0, blocks[c], lo:hi], in_=result[:])

@@ -81,7 +81,7 @@ def tile_attend_rate_topk_kernel(tc, qT, k_words, k_scales, kb, ex, offs, out):
 
         nc.sync.dma_start(offsets[:], offs)
         nc.sync.dma_start(out=scale_pool[0:SCALE_ROWS, :], in_=k_scales.bitcast(I32).rearrange("o f t -> f o t"))
-        nc.sync.dma_start(out=kb_pool[KB_ROW:P, :], in_=kb[0:1, :])
+        nc.scalar.dma_start(out=kb_pool[KB_ROW:P, :], in_=kb[0:1, :])
         nc.sync.dma_start(out=word_pool[:], in_=k_words[0].rearrange("p t b -> p (t b)").bitcast(I32))
         q_raw = []
         for o in range(PASSES):
@@ -207,11 +207,16 @@ def tile_attend_rate_topk_kernel(tc, qT, k_words, k_scales, kb, ex, offs, out):
             logit = sbuf([P, hi - lo], F32, f"logit{c}{lo}", RAW[1] + 4 * lo if c == 0 else None)
             rate = sbuf([P, hi - lo], F32, f"rate{c}{lo}")
             result = sbuf([P, hi - lo], F32, f"result{c}{lo}")
-            for j in range(lo // P, hi // P):
-                h, inside = divmod(j, PER_HALF)
-                cols = slice(j * P - lo, (j + 1) * P - lo)
+            step = P // 2 if (c, lo, hi) == PIECES[-1] else P
+            for first in range(lo, hi, step):
+                j, start = divmod(first, P)
+                h, inside = divmod(first, HALF)
+                cols = slice(first - lo, first - lo + step)
                 nc.vector.tensor_tensor(
-                    out=logit[:, cols], in0=scores[c, j][:], in1=bias[h][:, inside * P : (inside + 1) * P], op=ADD
+                    out=logit[:, cols],
+                    in0=scores[c, j][:, start : start + step],
+                    in1=bias[h][:, inside : inside + step],
+                    op=ADD,
                 )
                 nc.scalar.activation(out=rate[:, cols], in_=logit[:, cols], func=EXP)
             if (c, lo) == (0, 0):

@@ -35,7 +35,8 @@ QUADRANT = 32
 GROUP = 4
 SCALE_ROWS = PASSES * GROUP * GROUP
 KB_ROW = P - 1
-ODD_SPLIT = T // 2 + 1
+ON_VECTOR = 13 * T // 16
+ODD_SPLIT = ON_VECTOR // 2 + 1
 LINE = 4
 PIECES = ((0, 0, 256), (0, 256, 512), (1, 0, 256), (1, 256, 384), (1, 384, 512))
 
@@ -75,12 +76,13 @@ def tile_attend_rate_topk_kernel(tc, qT, k_words, k_scales, kb, ex, offs, out):
         nc.gpsimd.iota(distance[:], [[1, P]], base=0, channel_multiplier=-1, allow_small_or_imprecise_dtypes=True)
         nc.scalar.activation(out=apart[:], in_=distance[:], func=ABS)
         nc.scalar.activation(out=ident[:], in_=apart[:], func=RELU, scale=-1.0, bias=1.0)
+        nc.gpsimd.memset(kb_pool[0:KB_ROW, ON_VECTOR:T], 0.0)
         nc.gpsimd.memset(planes[:], 0)
         nc.vector.memset(kb_pool[0:KB_ROW, 0:ODD_SPLIT], 0.0)
-        nc.vector.memset(kb_pool[0:KB_ROW, ODD_SPLIT:T], 0.0)
+        nc.vector.memset(kb_pool[0:KB_ROW, ODD_SPLIT:ON_VECTOR], 0.0)
 
-        nc.sync.dma_start(offsets[:], offs)
         nc.sync.dma_start(out=scale_pool[0:SCALE_ROWS, :], in_=k_scales.bitcast(I32).rearrange("o f t -> f o t"))
+        nc.sync.dma_start(offsets[:], offs)
         nc.scalar.dma_start(out=kb_pool[KB_ROW:P, :], in_=kb[0:1, :])
         nc.sync.dma_start(out=word_pool[:], in_=k_words[0].rearrange("p t b -> p (t b)").bitcast(I32))
         q_raw = []

@@ -84,12 +84,12 @@ def tile_attend_rate_topk_kernel(tc, qT, k_words, k_scales, kb, ex, offs, out):
         nc.sync.dma_start(out=scale_pool[0:SCALE_ROWS, :], in_=k_scales.bitcast(I32).rearrange("o f t -> f o t"))
         nc.sync.dma_start(offsets[:], offs)
         nc.scalar.dma_start(out=kb_pool[KB_ROW:P, :], in_=kb[0:1, :])
-        nc.sync.dma_start(out=word_pool[:], in_=k_words[0].rearrange("p t b -> p (t b)").bitcast(I32))
+        nc.scalar.dma_start(out=word_pool[:], in_=k_words[0].rearrange("p t b -> p (t b)").bitcast(I32))
         q_raw = []
         for o in range(PASSES):
             q_raw.append(sbuf([P, PACK, NQ], F32, f"q_raw{o}", RAW[o]))
             rows = qT[0, o * K_PASS : (o + 1) * K_PASS, :]
-            nc.sync.dma_start(out=q_raw[o][:], in_=rows.rearrange("(p j) q -> p j q", j=PACK))
+            nc.scalar.dma_start(out=q_raw[o][:], in_=rows.rearrange("(p j) q -> p j q", j=PACK))
 
         listed_scales = sbuf([P, N], U8, "listed_scales")
         nc.vector.tensor_copy(out=listed_scales[:], in_=scale_pool[:].bitcast(U8).indirect(offsets[:]))

from contextlib import ExitStack

import concourse.mybir as mybir

T, D, NQ, N = 2048, 1024, 256, 512
FLOPS = 2 * NQ * N * D
BYTES = 4 * D * NQ + 4 * 128 * T + 32 * T + 4 * T + 4 * NQ + 2 * 128 * (N // 16) + 4 * NQ * N

F32 = mybir.dt.float32
BF16 = mybir.dt.bfloat16
I32 = mybir.dt.int32
U32 = mybir.dt.uint32
U16 = mybir.dt.uint16
U8 = mybir.dt.uint8
FP8X4 = mybir.dt.float8_e4m3fn_x4
FP4X4 = mybir.dt.float4_e2m1fn_x4
EXP = mybir.ActivationFunctionType.Exp
COPY = mybir.ActivationFunctionType.Copy
ABS = mybir.ActivationFunctionType.Abs
RELU = mybir.ActivationFunctionType.Relu
ADD = mybir.AluOpType.add
MULT = mybir.AluOpType.mult

P = 128
PACK = 4
K_PASS = P * PACK
PASSES = D // K_PASS
Q_BLOCKS = NQ // P
QUARTERS = N // P
HALVES = 2
HALF = N // HALVES
PER_HALF = QUARTERS // HALVES
LIST_GROUP = 16
QUADRANT = 32
GROUP = 4
SCALE_ROWS = PASSES * GROUP * GROUP
KB_ROW = P - 1
ON_VECTOR = 13 * T // 16
ODD_SPLIT = ON_VECTOR // 2 + 1
LINE = 4
PIECES = ((0, 0, 256), (0, 256, 512), (1, 0, 256), (1, 256, 384), (1, 384, 512))

KIB = 1024
FIRST_CHAIN = 0
SECOND_CHAIN = 1 * KIB
COLUMNS = 2 * KIB
RAW = (4 * KIB, 8 * KIB)


def tile_attend_rate_topk_kernel(tc, qT, k_words, k_scales, kb, ex, offs, out):
    nc = tc.nc
    with ExitStack() as ctx:
        keep = ctx.enter_context(tc.tile_pool(name="keep", bufs=1))
        shared = ctx.enter_context(tc.tile_pool(name="shared", bufs=1))
        psum = ctx.enter_context(tc.psum_pool(name="psum", bufs=1))

        def sbuf(shape, dtype, name, at=None):
            if at is None:
                return keep.tile(shape, dtype, name=name, align_bytes=64)
            return shared.tile(shape, dtype, name=name, offset=at, align_bytes=64)

        def bank(columns, name, number):
            return psum.tile([P, columns], F32, name=name, tag=f"bank{number}")

        offsets = keep.tile([P, N // LIST_GROUP], U16, name="offsets")
        scale_pool = sbuf([P, T // 4], I32, "scale_pool")
        kb_pool = sbuf([P, T], F32, "kb_pool")
        word_pool = sbuf([P, T], I32, "word_pool")
        ident = sbuf([P, P], F32, "ident")
        planes = sbuf([P, PASSES, N // 4], I32, "planes")

        nc.gpsimd.memset(scale_pool[SCALE_ROWS : P // 2, :], 0)
        nc.gpsimd.memset(scale_pool[P // 2 : P, :], 0)
        distance = sbuf([P, P], F32, "distance", FIRST_CHAIN)
        apart = sbuf([P, P], F32, "apart", SECOND_CHAIN)
        nc.gpsimd.iota(distance[:], [[1, P]], base=0, channel_multiplier=-1, allow_small_or_imprecise_dtypes=True)
        nc.scalar.activation(out=apart[:], in_=distance[:], func=ABS)
        nc.scalar.activation(out=ident[:], in_=apart[:], func=RELU, scale=-1.0, bias=1.0)
        nc.gpsimd.memset(kb_pool[0:KB_ROW, ON_VECTOR:T], 0.0)
        nc.gpsimd.memset(planes[:], 0)
        nc.vector.memset(kb_pool[0:KB_ROW, 0:ODD_SPLIT], 0.0)
        nc.vector.memset(kb_pool[0:KB_ROW, ODD_SPLIT:ON_VECTOR], 0.0)

        nc.sync.dma_start(out=scale_pool[0:SCALE_ROWS, :], in_=k_scales.bitcast(I32).rearrange("o f t -> f o t"))
        nc.sync.dma_start(offsets[:], offs)
        nc.scalar.dma_start(out=kb_pool[KB_ROW:P, :], in_=kb[0:1, :])
        nc.scalar.dma_start(out=word_pool[:], in_=k_words[0].rearrange("p t b -> p (t b)").bitcast(I32))
        q_raw = []
        for o in range(PASSES):
            q_raw.append(sbuf([P, PACK, NQ], F32, f"q_raw{o}", RAW[o]))
            rows = qT[0, o * K_PASS : (o + 1) * K_PASS, :]
            nc.scalar.dma_start(out=q_raw[o][:], in_=rows.rearrange("(p j) q -> p j q", j=PACK))

        listed_scales = sbuf([P, N], U8, "listed_scales")
        nc.vector.tensor_copy(out=listed_scales[:], in_=scale_pool[:].bitcast(U8).indirect(offsets[:]))
        for g in range(GROUP):
            source = slice(PASSES * GROUP * g, PASSES * GROUP * (g + 1))
            nc.sync.dma_start(
                out=planes[QUADRANT * g : QUADRANT * g + GROUP, :, :], in_=listed_scales[source, :].bitcast(I32)
            )
        key_scales = [planes[:, o, :].bitcast(U8) for o in range(PASSES)]

        entries = [offsets[:, h * HALF // LIST_GROUP : (h + 1) * HALF // LIST_GROUP] for h in range(HALVES)]
        slots = [slice(h * HALF, (h + 1) * HALF) for h in range(HALVES)]
        blocks = [slice(c * P, (c + 1) * P) for c in range(Q_BLOCKS)]

        kb_row = [sbuf([P, HALF], F32, f"kb_row{h}", (FIRST_CHAIN, SECOND_CHAIN)[h]) for h in range(HALVES)]
        for h in range(HALVES):
            nc.scalar.activation(out=kb_row[h][:], in_=kb_pool[:].indirect(entries[h]), func=COPY)

        turned = []
        for h in range(HALVES):
            turned.append(bank(HALF, f"turned{h}", QUARTERS + h))
            for j in range(PER_HALF):
                nc.tensor.transpose(turned[h][:, j * P : (j + 1) * P], kb_row[h][:, j * P : (j + 1) * P], ident[:])

        def bias_columns(h, copy, at=None):
            columns = sbuf([P, PER_HALF], F32, f"kb_cols{h}", at)
            copy(out=columns[:], in_=turned[h][:].rearrange("p (j r) -> p j r", r=P)[:, :, KB_ROW])
            return columns

        def spread(rows, columns, j):
            nc.tensor.transpose(rows, columns[:, j : j + 1].to_broadcast([P, P]), ident[:])

        first_columns = bias_columns(0, nc.scalar.copy, COLUMNS)
        first_spread = bank(HALF, "first_spread", QUARTERS)
        for j in range(PER_HALF):
            spread(first_spread[:, j * P : (j + 1) * P], first_columns, j)

        exposure = sbuf([P, Q_BLOCKS], F32, "exposure", COLUMNS)
        with nc.allow_non_contiguous_dma(reason="one exposure a query row"):
            nc.sync.dma_start(out=exposure[:], in_=ex[0].rearrange("(c p) one -> p (c one)", p=P))

        word_pairs = sbuf([P, N], U32, "word_pairs")
        for h in range(HALVES):
            nc.vector.tensor_copy(out=word_pairs[:, slots[h]], in_=word_pool[:].bitcast(U32).indirect(entries[h]))
        by_pass = word_pairs[:].bitcast(U16).rearrange("p (i o) -> p o i", o=PASSES)

        key_words, quantised, scores = {}, {}, {}

        def part(o, h, at=None):
            key_words[o, h] = sbuf([P, 2 * HALF], U8, f"key_words{o}{h}", at)
            nc.vector.tensor_copy(out=key_words[o, h][:].bitcast(U16), in_=by_pass[:, o, slots[h]])

        def round_queries(o, c, copy, at):
            q_bf = sbuf([P, P, PACK], BF16, f"q_bf{o}{c}", at)
            copy(
                out=q_bf[:].rearrange("p (a i) j -> p a j i", i=LINE),
                in_=q_raw[o][:, :, blocks[c]].rearrange("p j (a i) -> p a j i", i=LINE),
            )
            return q_bf

        def quantise(o, c, q_bf, at=None):
            q_codes = sbuf([P, P], U32, f"q_codes{o}{c}", at)
            q_scales = sbuf([P, P], U8, f"q_scales{o}{c}")
            nc.vector.quantize_mx(
                out=q_codes[:].bitcast(FP8X4), scales=q_scales[:], in_=q_bf[:].rearrange("p q j -> p (q j)")
            )
            quantised[o, c] = (q_codes, q_scales)

        def score(o, c, quarters):
            q_codes, q_scales = quantised[o, c]
            for j in quarters:
                if o == 0:
                    scores[c, j] = bank(P, f"scores{c}{j}", QUARTERS * c + j)
                h, inside = divmod(j, PER_HALF)
                nc.tensor.matmul_mx(
                    out=scores[c, j][:],
                    lhsT=q_codes[:].bitcast(FP8X4),
                    lhsT_scale=q_scales[:],
                    rhs=key_words[o, h][:, 2 * inside * P : 2 * (inside + 1) * P].bitcast(FP4X4),
                    rhs_scale=key_scales[o][:, j * P : (j + 1) * P],
                    start=(o == 0),
                    stop=(o == PASSES - 1),
                )

        every = range(QUARTERS)
        late = every[PER_HALF:]
        for h in range(HALVES):
            part(0, h)

        rounded_00 = round_queries(0, 0, nc.scalar.copy, FIRST_CHAIN)
        second_columns = bias_columns(1, nc.vector.tensor_copy)
        second_spread = [bank(P, f"second_spread{j}", QUARTERS + j) for j in late]
        for j in range(PER_HALF):
            spread(second_spread[j][:], second_columns, j)
        bias = [sbuf([P, HALF], F32, "bias0")]
        nc.scalar.copy(out=bias[0][:], in_=first_spread[:])
        rounded_01 = round_queries(0, 1, nc.vector.tensor_copy, SECOND_CHAIN)
        quantise(0, 0, rounded_00)
        score(0, 0, every)

        rounded_10 = round_queries(1, 0, nc.vector.tensor_copy, RAW[0])
        part(1, 0, RAW[0] + KIB + KIB // 2)
        quantise(1, 0, rounded_10)
        part(1, 1, RAW[0] + KIB)
        score(1, 0, every)
        quantise(0, 1, rounded_01, RAW[0])
        rounded_11 = round_queries(1, 1, nc.scalar.copy, RAW[0] + 2 * KIB)
        quantise(1, 1, rounded_11)
        bias.append(sbuf([P, HALF], F32, "bias1", RAW[1] + 2 * KIB))
        for j in range(PER_HALF):
            nc.scalar.copy(out=bias[1][:, j * P : (j + 1) * P], in_=second_spread[j][:])
        for j in every:
            for o in range(PASSES):
                score(o, 1, [j])

        for c, lo, hi in PIECES:
            logit = sbuf([P, hi - lo], F32, f"logit{c}{lo}", RAW[1] + 4 * lo if c == 0 else None)
            rate = sbuf([P, hi - lo], F32, f"rate{c}{lo}")
            result = sbuf([P, hi - lo], F32, f"result{c}{lo}")
            step = P // 2 if (c, lo, hi) == PIECES[-1] else P
            for first in range(lo, hi, step):
                j, start = divmod(first, P)
                h, inside = divmod(first, HALF)
                cols = slice(first - lo, first - lo + step)
                nc.vector.tensor_tensor(
                    out=logit[:, cols],
                    in0=scores[c, j][:, start : start + step],
                    in1=bias[h][:, inside : inside + step],
                    op=ADD,
                )
                nc.scalar.activation(out=rate[:, cols], in_=logit[:, cols], func=EXP)
            if (c, lo) == (0, 0):
                nc.gpsimd.tensor_scalar(
                    out=result[:], in0=rate[:], scalar1=exposure[:, 0:1], scalar2=0.0, op0=MULT, op1=ADD
                )
            else:
                nc.vector.tensor_scalar_mul(out=result[:], in0=rate[:], scalar1=exposure[:, c : c + 1])
            nc.sync.dma_start(out=out[0, blocks[c], lo:hi], in_=result[:])
